import numpy as np
import ml_dtypes


def mxq(x, axis, fmt="e4m3"):
    dtype, down = {"e4m3": (ml_dtypes.float8_e4m3fn, 7), "e5m2": (ml_dtypes.float8_e5m2, 14)}[fmt]
    v = np.moveaxis(np.asarray(x, np.float32).astype(ml_dtypes.bfloat16).astype(np.float64), axis, -1)
    blocks = v.reshape(v.shape[:-1] + (-1, 32))
    amax = np.abs(blocks).max(-1, keepdims=True)
    byte = np.maximum(np.where(amax > 0, np.frexp(amax)[1] - 1 + 127, 0) - down, 1)
    scale = np.exp2(byte - 127.0)
    codes = (blocks / scale).astype(np.float32).astype(dtype).astype(np.float64)
    return np.moveaxis((codes * scale).reshape(v.shape), -1, axis)


WIDE = False


def mx_kscale(k):
    if not WIDE:
        return np.ones(k)
    levels = np.array([10, -10, 5, -5, 0])
    if k % 512:
        return np.exp2(np.random.permutation(np.resize(levels, k // 32))).repeat(32)
    a = np.empty((k // 512, 16))
    for p in range(k // 512):
        a[p, :8] = np.random.permutation(np.resize(levels, 8))
        for g in range(8):
            far = levels[np.abs(levels - a[p, g]) >= 10]
            a[p, g + 8] = far[np.random.randint(len(far))]
    return np.exp2(a.ravel()).repeat(32)


BF16 = ml_dtypes.bfloat16


def bf(x):
    return np.asarray(x, np.float32).astype(BF16)


def f64(x):
    return np.asarray(x).astype(np.float64)


N, D, H = 8192, 1024, 128
G = 2 * H


def sigmoid(v):
    return 1.0 / (1.0 + np.exp(-v))


def mogrify(x, h, q):
    a = h @ q
    return 2.0 * sigmoid(a) * x


def draw0():
    t = mx_kscale(D)
    return {
        "x": bf(np.random.standard_normal((N, D)) * t),
        "h": bf(np.random.standard_normal((N, H))),
        "c": bf(np.random.standard_normal((N, H))),
        "q": bf(np.random.standard_normal((H, D)) / np.sqrt(H)),
        "w": bf(np.random.standard_normal((D, G)) / np.sqrt(D) / t[:, None]),
        "u": bf(np.random.standard_normal((H, G)) / np.sqrt(H)),
        "b": bf(np.random.standard_normal(G) * 0.3),
    }


def core(x, h, c, q, w, u, b):
    hidden = h.shape[1]
    x1 = mogrify(f64(x), f64(h), f64(q))
    pre = (mxq(x1, 1, "e4m3") @ mxq(f64(w), 0, "e4m3")) + f64(h) @ f64(u) + f64(b)
    pi = pre[:, 0:hidden]
    pg = pre[:, hidden:2 * hidden]
    i = sigmoid(pi)
    g = np.tanh(pg)
    return (1.0 - i) * f64(c) + i * g


def e4m3fn_bytes(y):
    return np.clip(np.asarray(y, np.float64), -448.0, 448.0).astype(np.float32).astype(ml_dtypes.float8_e4m3fn).view(np.uint8)


def e4m3fn_values(b):
    return np.asarray(b, np.uint8).view(ml_dtypes.float8_e4m3fn).astype(np.float64)


def setup_inputs():
    d = draw0()
    x0 = np.asarray(d['w']).astype(np.float64)
    s = (np.max(np.abs(x0), axis=(1,), keepdims=True) / 448.0).astype(np.float32)
    out = {}
    for k, v in d.items():
        if k == 'w':
            out['w_bytes'] = e4m3fn_bytes(x0 / s.astype(np.float64))
            out['w_scale'] = s
        else:
            out[k] = v
    return out


def reference(x, h, c, q, w_bytes, w_scale, u, b):
    return core(x, h, c, q, e4m3fn_values(w_bytes) * w_scale.astype(np.float64), u, b)

@@ -1,0 +1,314 @@
+from contextlib import ExitStack
+
+import concourse.mybir as mybir
+from concourse.masks import make_identity
+
+F32 = mybir.dt.float32
+BF16 = mybir.dt.bfloat16
+U32 = mybir.dt.uint32
+U8 = mybir.dt.uint8
+FP8 = mybir.dt.float8_e4m3fn
+FP8X4 = mybir.dt.float8_e4m3fn_x4
+ACT = mybir.ActivationFunctionType
+ALU = mybir.AluOpType
+
+P = 128
+N, D, H = 8192, 1024, 128
+G = 2 * H
+NT = N // P
+NP = NT // 2
+PACK = 4
+NG = D // (P * PACK)
+FLOPS = 2 * N * (H * D + H * G + D * G)
+MIX = False
+
+
+def tile_mogrifieroneroundcoupledlstmcell_t_kernel(tc, x, h, c, q, w_bytes, w_scale, u, b, out):
+    nc = tc.nc
+    xv = x.rearrange("(p j) d -> p j d", p=P)
+    hv = h.rearrange("(p j) d -> p j d", p=P)
+    cv = c.rearrange("(p j) d -> p j d", p=P)
+    ov = out.rearrange("(p j) d -> p j d", p=P)
+    with ExitStack() as ctx:
+        const = ctx.enter_context(tc.tile_pool(name="const", bufs=1))
+        xin = ctx.enter_context(tc.tile_pool(name="xin", bufs=8))
+        work = ctx.enter_context(tc.tile_pool(name="work", bufs=4))
+        ps_a = ctx.enter_context(tc.psum_pool(name="ps_a", bufs=3))
+        ps_x = ctx.enter_context(tc.psum_pool(name="ps_x", bufs=2))
+        ps_h = ctx.enter_context(tc.psum_pool(name="ps_h", bufs=1))
+        ps_p = ctx.enter_context(tc.psum_pool(name="ps_p", bufs=1))
+        ps_u = ctx.enter_context(tc.psum_pool(name="ps_u", bufs=1)) if not MIX else None
+
+        ident_f = const.tile([P, P], F32, name="ident_f")
+        ident_b = const.tile([P, P], BF16, name="ident_b")
+        ones = const.tile([P, P], BF16, name="ones")
+        brow = const.tile([P, G], BF16, name="brow")
+        q_raw = const.tile([P, D], BF16, name="q_raw")
+        q_sb = const.tile([P, NG, PACK, P], BF16, name="q_sb")
+        u_sb = const.tile([P, G], BF16, name="u_sb")
+        w_raw = const.tile([P, NG, PACK, G], U8, name="w_raw", align_bytes=64)
+        w_sc = const.tile([P, NG, PACK], F32, name="w_sc")
+        w_f32 = const.tile([P, PACK, G], F32, name="w_f32")
+        w_wide = const.tile([P, NG, PACK, G], BF16, name="w_wide")
+        w_grp = const.tile([P, NG, G, PACK], BF16, name="w_grp", align_bytes=64)
+        w_codes = const.tile([P, NG * G], U32, name="w_codes", align_bytes=64)
+        w_scales = const.tile([P, NG * G], U8, name="w_scales", align_bytes=64)
+        warm = const.tile([P, 1], F32, name="warm")
+
+        hs = {}
+        cs = {}
+        xs = {}
+        HC = 4
+
+        def load_h(k):
+            t = const.tile([P, HC, H], BF16, name="h%d" % k)
+            nc.sync.dma_start(out=t[:], in_=hv[:, HC * k : HC * k + HC, :])
+            hs[k] = t
+
+        def load_hc(k0, k1):
+            t = const.tile([P, (k1 - k0) * HC, H], BF16, name="h%d" % k0)
+            nc.sync.dma_start(out=t[:], in_=hv[:, HC * k0 : HC * k1, :])
+            for k in range(k0, k1):
+                hs[k] = (t, (k - k0) * HC)
+
+        def load_c(k0, k1):
+            t = const.tile([P, (k1 - k0) * 2, H], BF16, name="c%d" % k0)
+            nc.sync.dma_start(out=t[:], in_=cv[:, 2 * k0 : 2 * k1, :])
+            for k in range(k0, k1):
+                cs[k] = (t, (k - k0) * 2)
+
+        def load_x(i):
+            t = xin.tile([P, 2, D], BF16, name="x_in")
+            nc.sync.dma_start(out=t[:], in_=xv[:, 2 * i : 2 * i + 2, :])
+            xs[i] = t
+
+        nc.vector.memset(warm[:], 0.0)
+        nc.scalar.activation(out=warm[:], in_=warm[:], func=ACT.Sigmoid)
+        make_identity(nc, ident_b[:])
+        make_identity(nc, ident_f[:])
+        load_hc(0, 1)
+        nc.sync.dma_start(out=q_raw[:], in_=q)
+        nc.sync.dma_start(out=w_raw[:], in_=w_bytes.rearrange("(g p t) n -> p g t n", p=P, t=PACK))
+        load_x(0)
+        nc.sync.dma_start(out=u_sb[:], in_=u)
+        nc.vector.memset(brow[:], 0.0)
+        nc.vector.memset(ones[:], 1.0)
+        nc.sync.dma_start(out=brow[0:1, :], in_=b.rearrange("(o n) -> o n", o=1))
+        nc.sync.dma_start(out=w_sc[:], in_=w_scale.rearrange("(g p t) o -> p g (t o)", p=P, t=PACK))
+        load_x(1)
+        load_hc(1, 4)
+        load_x(2)
+        load_c(0, 4)
+        load_x(3)
+
+        ht = {}
+        st = {}
+        x1s = {}
+        cod = {}
+        pre = {}
+        hub = {}
+        gates_in = {}
+        outs = {}
+
+        def pe_h(k):
+            t, o = hs[k]
+            hp = ps_h.tile([P, 4, P], BF16, name="hp")
+            for j in range(4):
+                nc.tensor.transpose(hp[:, j, :], t[:, o + j, :], ident_b[:])
+            ht[k] = [hp, None]
+
+        def copy_h(k):
+            s = work.tile([P, 4, P], BF16, name="hT")
+            nc.scalar.copy(out=s[:], in_=ht[k][0][:])
+            ht[k][1] = s
+
+        def hT(i, jj):
+            return ht[i // 2][1][:, 2 * (i % 2) + jj, :]
+
+        def pe_a(i, g, jj):
+            a = ps_a.tile([P, PACK, P], F32, name="aT")
+            for t in range(PACK):
+                nc.tensor.matmul(a[:, t, :], lhsT=q_sb[:, g, t, :], rhs=hT(i, jj), start=True, stop=True)
+            st[(i, g, jj)] = a
+
+        def pe_x(i, g):
+            xp = ps_x.tile([P, 2 * P, 2], F32, name="xT")
+            words = xs[i][:].bitcast(F32)
+            for jj in range(2):
+                for v in range(2):
+                    nc.tensor.transpose(
+                        xp[:, P * jj : P * jj + P, v],
+                        words[:, jj, 256 * g + v : 256 * g + 256 : 2],
+                        ident_f[:],
+                    )
+            st[("x", i, g)] = xp
+
+        def pe_hu(i):
+            hp = ps_u.tile([P, 2, G], F32, name="hu")
+            for jj in range(2):
+                nc.tensor.matmul(hp[:, jj, :], lhsT=hT(i, jj), rhs=u_sb[:], start=True, stop=False)
+                nc.tensor.matmul(hp[:, jj, :], lhsT=ones[:], rhs=brow[:], start=False, stop=True)
+            hub[i] = hp
+
+        def pe_mx(i):
+            pt = ps_p.tile([P, 2, G], F32, name="pre")
+            co, sc = cod[i]
+            for jj in range(2):
+                if MIX:
+                    nc.tensor.matmul(pt[:, jj, :], lhsT=hT(i, jj), rhs=u_sb[:], start=True, stop=False)
+                for g in range(NG):
+                    cols = slice(g * 256 + jj * P, g * 256 + jj * P + P)
+                    nc.tensor.matmul_mx(
+                        out=pt[:, jj, :],
+                        lhsT=co[:, cols].bitcast(FP8X4),
+                        lhsT_scale=sc[:, cols],
+                        rhs=w_codes[:, g * G : g * G + G].bitcast(FP8X4),
+                        rhs_scale=w_scales[:, g * G : g * G + G],
+                        start=(g == 0 and not MIX),
+                        stop=(g == NG - 1 and not MIX),
+                    )
+                if MIX:
+                    nc.tensor.matmul(pt[:, jj, :], lhsT=ones[:], rhs=brow[:], start=False, stop=True)
+            pre[i] = pt
+
+        def act_sig(i, g, jj):
+            if jj == 0:
+                st[("s", i, g)] = work.tile([P, 2, P, PACK], F32, name="sg")
+            s = st[("s", i, g)]
+            nc.scalar.activation(
+                out=s[:, jj, :, :], in_=st[(i, g, jj)][:].rearrange("p t n -> p n t"), func=ACT.Sigmoid
+            )
+
+        def act_hu(i):
+            s = work.tile([P, 2, G], F32, name="hub")
+            nc.scalar.copy(out=s[:], in_=hub[i][:])
+            hub[i] = s
+
+        def act_gates(i):
+            src = pre[i] if MIX else gates_in[i]
+            gi = work.tile([P, 2, H], F32, name="gi")
+            gg = work.tile([P, 2, H], F32, name="gg")
+            nc.scalar.activation(out=gg[:], in_=src[:, :, H:G], func=ACT.Tanh)
+            nc.scalar.activation(out=gi[:], in_=src[:, :, 0:H], func=ACT.Sigmoid)
+            outs[i] = (gi, gg)
+
+        def dve_mult(i, g):
+            if g == 0:
+                x1s[i] = work.tile([P, NG, 1024], BF16, name="x1", align_bytes=64)
+            nc.vector.scalar_tensor_tensor(
+                out=x1s[i][:, g, :],
+                in0=st[("x", i, g)][:].rearrange("p n v -> p (n v)").bitcast(BF16),
+                scalar=2.0,
+                in1=st[("s", i, g)][:].rearrange("p j n t -> p (j n t)"),
+                op0=ALU.mult,
+                op1=ALU.mult,
+            )
+
+        def dve_quant(i):
+            co = work.tile([P, 512], U32, name="codes", align_bytes=64)
+            sc = work.tile([P, 512], U8, name="scales", align_bytes=64)
+            nc.vector.quantize_mx(
+                out=co[:].bitcast(FP8X4), scales=sc[:], in_=x1s[i][:].rearrange("p g m -> p (g m)")
+            )
+            cod[i] = (co, sc)
+
+        def dve_add(i):
+            s = work.tile([P, 2, G], F32, name="pre_sb")
+            nc.vector.tensor_tensor(out=s[:], in0=pre[i][:], in1=hub[i][:], op=ALU.add)
+            gates_in[i] = s
+
+        def fin(i):
+            gi, gg = outs[i]
+            t, o = cs[i]
+            cc = t[:, o : o + 2, :]
+            ob = work.tile([P, 2, H], F32, name="ob")
+            e = nc.vector if i == NP - 1 else nc.gpsimd
+            e.tensor_tensor(out=gg[:], in0=gg[:], in1=cc, op=ALU.subtract)
+            e.tensor_tensor(out=gi[:], in0=gi[:], in1=gg[:], op=ALU.mult)
+            e.tensor_tensor(out=ob[:], in0=gi[:], in1=cc, op=ALU.add)
+            nc.sync.dma_start(out=ov[:, 2 * i : 2 * i + 2, :], in_=ob[:])
+
+        with tc.manual_schedule():
+            pe_h(0)
+            copy_h(0)
+            qv = q_raw[:].rearrange("k (g p t) -> k g t p", p=P, t=PACK)
+            nc.vector.tensor_copy(out=q_sb[:, 0, :, :], in_=qv[:, 0, :, :])
+            nc.vector.tensor_copy(out=q_sb[:, 1, :, :], in_=qv[:, 1, :, :])
+            for t in range(PACK):
+                nc.vector.tensor_scalar(
+                    out=w_wide[:, 0, t, :],
+                    in0=w_raw[:, 0, t, :].bitcast(FP8),
+                    scalar1=w_sc[:, 0, t : t + 1],
+                    scalar2=None,
+                    op0=ALU.mult,
+                )
+            nc.vector.tensor_copy(out=w_grp[:, 0, :, :], in_=w_wide[:, 0, :, :].rearrange("p t n -> p n t"))
+            nc.gpsimd.tensor_copy(out=w_f32[:], in_=w_raw[:, 1, :, :].bitcast(FP8))
+            for t in range(PACK):
+                nc.gpsimd.tensor_scalar(
+                    out=w_wide[:, 1, t, :],
+                    in0=w_f32[:, t, :],
+                    scalar1=w_sc[:, 1, t : t + 1],
+                    scalar2=0.0,
+                    op0=ALU.mult,
+                    op1=ALU.add,
+                )
+            nc.gpsimd.tensor_scalar(
+                out=w_grp[:, 1, :, :],
+                in0=w_wide[:, 1, :, :].rearrange("p t n -> p n t"),
+                scalar1=1.0,
+                scalar2=0.0,
+                op0=ALU.mult,
+                op1=ALU.add,
+            )
+            for i in range(NP + 4):
+                if i + 4 < NP:
+                    load_x(i + 4)
+                    if i == 2:
+                        load_hc(4, 10)
+                    if i == 4:
+                        load_c(4, 16)
+                    if i == 8:
+                        load_hc(10, 16)
+                    if i == 10:
+                        load_c(16, 32)
+                if i < NP:
+                    pe_a(i, 0, 0)
+                    pe_x(i, 0)
+                    pe_a(i, 0, 1)
+                    if not MIX:
+                        pe_hu(i)
+                    pe_a(i, 1, 0)
+                    pe_x(i, 1)
+                    pe_a(i, 1, 1)
+                if i % 2 == 0 and i // 2 + 1 < NP // 2:
+                    pe_h(i // 2 + 1)
+                if 0 <= i - 2 < NP:
+                    pe_mx(i - 2)
+                if i < NP:
+                    act_sig(i, 0, 0)
+                    act_sig(i, 0, 1)
+                    if not MIX:
+                        act_hu(i)
+                    act_sig(i, 1, 0)
+                    act_sig(i, 1, 1)
+                if 0 <= i - 3 < NP:
+                    act_gates(i - 3)
+                if i < NP:
+                    dve_mult(i, 0)
+                if 0 <= i - 1 < NP:
+                    dve_quant(i - 1)
+                if i % 2 == 0 and i // 2 + 1 < NP // 2:
+                    copy_h(i // 2 + 1)
+                if i < NP:
+                    dve_mult(i, 1)
+                if i == 1:
+                    nc.vector.quantize_mx(
+                        out=w_codes[:].bitcast(FP8X4),
+                        scales=w_scales[:],
+                        in_=w_grp[:].rearrange("p g n t -> p (g n t)"),
+                    )
+                if not MIX and 0 <= i - 2 < NP:
+                    dve_add(i - 2)
+                if 0 <= i - 3 < NP:
+                    fin(i - 3)

@@ -16,11 +16,12 @@ P = 128
 N, D, H = 8192, 1024, 128
 G = 2 * H
 NT = N // P
-NP = NT // 2
+NQ = NT // 4
 PACK = 4
 NG = D // (P * PACK)
 FLOPS = 2 * N * (H * D + H * G + D * G)
-MIX = False
+GROUPS = [(4 * i, 4) for i in range(NQ - 1)] + [(NT - 4, 2), (NT - 2, 2)]
+I_HALF, G_HALF = 0, 1
 
 
 def tile_mogrifieroneroundcoupledlstmcell_t_kernel(tc, x, h, c, q, w_bytes, w_scale, u, b, out):
@@ -30,285 +31,304 @@ def tile_mogrifieroneroundcoupledlstmcell_t_kernel(tc, x, h, c, q, w_bytes, w_sc
     cv = c.rearrange("(p j) d -> p j d", p=P)
     ov = out.rearrange("(p j) d -> p j d", p=P)
     with ExitStack() as ctx:
-        const = ctx.enter_context(tc.tile_pool(name="const", bufs=1))
-        xin = ctx.enter_context(tc.tile_pool(name="xin", bufs=8))
-        work = ctx.enter_context(tc.tile_pool(name="work", bufs=4))
+        keep = ctx.enter_context(tc.tile_pool(name="keep", bufs=1))
+        xin = ctx.enter_context(tc.tile_pool(name="xin", bufs=6))
+        work = ctx.enter_context(tc.tile_pool(name="work", bufs=3))
+        sgp = ctx.enter_context(tc.tile_pool(name="sgp", bufs=4))
         ps_a = ctx.enter_context(tc.psum_pool(name="ps_a", bufs=3))
-        ps_x = ctx.enter_context(tc.psum_pool(name="ps_x", bufs=2))
-        ps_h = ctx.enter_context(tc.psum_pool(name="ps_h", bufs=1))
-        ps_p = ctx.enter_context(tc.psum_pool(name="ps_p", bufs=1))
-        ps_u = ctx.enter_context(tc.psum_pool(name="ps_u", bufs=1)) if not MIX else None
+        ps_x = ctx.enter_context(tc.psum_pool(name="ps_x", bufs=3))
+        ps_m = ctx.enter_context(tc.psum_pool(name="ps_m", bufs=1))
+        ps_s = ctx.enter_context(tc.psum_pool(name="ps_s", bufs=1))
 
-        ident_f = const.tile([P, P], F32, name="ident_f")
-        ident_b = const.tile([P, P], BF16, name="ident_b")
-        ones = const.tile([P, P], BF16, name="ones")
-        brow = const.tile([P, G], BF16, name="brow")
-        q_raw = const.tile([P, D], BF16, name="q_raw")
-        q_sb = const.tile([P, NG, PACK, P], BF16, name="q_sb")
-        u_sb = const.tile([P, G], BF16, name="u_sb")
-        w_raw = const.tile([P, NG, PACK, G], U8, name="w_raw", align_bytes=64)
-        w_sc = const.tile([P, NG, PACK], F32, name="w_sc")
-        w_f32 = const.tile([P, PACK, G], F32, name="w_f32")
-        w_wide = const.tile([P, NG, PACK, G], BF16, name="w_wide")
-        w_grp = const.tile([P, NG, G, PACK], BF16, name="w_grp", align_bytes=64)
-        w_codes = const.tile([P, NG * G], U32, name="w_codes", align_bytes=64)
-        w_scales = const.tile([P, NG * G], U8, name="w_scales", align_bytes=64)
-        warm = const.tile([P, 1], F32, name="warm")
+        ident_f = keep.tile([P, P], F32, name="ident_f")
+        ident_b = keep.tile([P, P], BF16, name="ident_b")
+        b_row = keep.tile([P, P], BF16, name="b_row")
+        b_col = keep.tile([P, 2], F32, name="b_col")
+        q_raw = keep.tile([P, D], BF16, name="q_raw")
+        q_sb = keep.tile([P, NG, PACK, P], BF16, name="q_sb")
+        u_sb = keep.tile([P, G], BF16, name="u_sb")
+        w_raw = keep.tile([P, NG, PACK, G], U8, name="w_raw", align_bytes=64)
+        w_sc = keep.tile([P, NG, PACK], F32, name="w_sc")
+        w_wide = keep.tile([P, NG, PACK, G], BF16, name="w_wide")
+        w_grp = keep.tile([P, NG, G, PACK], BF16, name="w_grp", align_bytes=64)
+        w_codes = keep.tile([P, NG * G], U32, name="w_codes", align_bytes=64)
+        w_scales = keep.tile([P, NG * G], U8, name="w_scales", align_bytes=64)
+        warm = keep.tile([P, 1], F32, name="warm")
 
-        hs = {}
-        cs = {}
-        xs = {}
-        HC = 4
+        h_in, c_in, x_in, h_ps, h_t, a_ps, x_ps, sg, x1, codes, mx_ps, pre_t, pre_ps, gates = ({} for k in range(14))
 
-        def load_h(k):
-            t = const.tile([P, HC, H], BF16, name="h%d" % k)
-            nc.sync.dma_start(out=t[:], in_=hv[:, HC * k : HC * k + HC, :])
-            hs[k] = t
+        def load_h(lo, hi):
+            t = keep.tile([P, (hi - lo) * 4, H], BF16, name="h%d" % lo)
+            nc.sync.dma_start(out=t[:], in_=hv[:, 4 * lo : 4 * hi, :])
+            for i in range(lo, hi):
+                h_in[i] = t[:, 4 * (i - lo) : 4 * (i - lo) + 4, :]
 
-        def load_hc(k0, k1):
-            t = const.tile([P, (k1 - k0) * HC, H], BF16, name="h%d" % k0)
-            nc.sync.dma_start(out=t[:], in_=hv[:, HC * k0 : HC * k1, :])
-            for k in range(k0, k1):
-                hs[k] = (t, (k - k0) * HC)
+        def load_c(lo, hi):
+            t = keep.tile([P, (hi - lo) * 4, H], BF16, name="c%d" % lo)
+            nc.sync.dma_start(out=t[:], in_=cv[:, 4 * lo : 4 * hi, :])
+            for i in range(4 * lo, 4 * hi):
+                c_in[i] = (t, i - 4 * lo)
 
-        def load_c(k0, k1):
-            t = const.tile([P, (k1 - k0) * 2, H], BF16, name="c%d" % k0)
-            nc.sync.dma_start(out=t[:], in_=cv[:, 2 * k0 : 2 * k1, :])
-            for k in range(k0, k1):
-                cs[k] = (t, (k - k0) * 2)
-
-        def load_x(i):
+        def load_x(i, pieces=1):
             t = xin.tile([P, 2, D], BF16, name="x_in")
-            nc.sync.dma_start(out=t[:], in_=xv[:, 2 * i : 2 * i + 2, :])
-            xs[i] = t
+            w = 2 // pieces
+            for k in range(0, 2, w):
+                nc.sync.dma_start(out=t[:, k : k + w, :], in_=xv[:, 2 * i + k : 2 * i + k + w, :])
+            x_in[i] = t
+
+        def h_turn(i):
+            t = ps_x.tile([P, 4, P], BF16, name="xT")
+            for j in range(4):
+                nc.tensor.transpose(t[:, j, :], h_in[i][:, j, :], ident_b[:])
+            h_ps[i] = t
+
+        def h_copy(i, engine_copy):
+            t = keep.tile([P, 4, P], BF16, name="ht%d" % i)
+            engine_copy(out=t[:], in_=h_ps[i][:])
+            for j in range(4):
+                h_t[4 * i + j] = t[:, j, :]
+
+        def a_mm(i, k):
+            tile, g = 4 * i + 2 * (k // 4) + k % 2, k // 2 % 2
+            t = ps_a.tile([P, PACK, P], F32, name="aT")
+            for m in range(PACK):
+                nc.tensor.matmul(t[:, m, :], lhsT=q_sb[:, g, m, :], rhs=h_t[tile], start=True, stop=True)
+            a_ps[(i, k)] = t
+
+        def x_turn(i, k):
+            pair, g = 2 * i + k // 2, k % 2
+            t = ps_x.tile([P, 2, 2 * P], F32, name="xT")
+            words = x_in[pair][:].bitcast(F32)
+            for j in range(2):
+                for m in range(2):
+                    nc.tensor.transpose(
+                        t[:, m, P * j : P * j + P], words[:, j, 256 * g + m : 256 * g + 256 : 2], ident_f[:]
+                    )
+            x_ps[(i, k)] = t
+
+        def sig(i, k):
+            if k % 2 == 0:
+                sg[(i, k // 2)] = sgp.tile([P, 2, P, PACK], F32, name="sg")
+            nc.scalar.activation(
+                out=sg[(i, k // 2)][:, k % 2, :, :],
+                in_=a_ps[(i, k)][:].rearrange("p m n -> p n m"),
+                func=ACT.Sigmoid,
+            )
+
+        def mult(i, k):
+            pair, g = k // 2, k % 2
+            j, slot = (i, pair) if i < NQ - 1 else (NQ - 1 + pair, 0)
+            if j not in x1:
+                x1[j] = work.tile([P, NG, GROUPS[j][1] * 512], BF16, name="x1", align_bytes=64)
+            nc.vector.tensor_tensor(
+                out=x1[j][:, g, 1024 * slot : 1024 * slot + 1024].rearrange("p (n m e) -> p n m e", m=2, e=2),
+                in0=x_ps[(i, k)][:].bitcast(BF16).rearrange("p m (n e) -> p n m e", e=2),
+                in1=sg[(i, k)][:].rearrange("p j n (m e) -> p (j n) m e", m=2),
+                op=ALU.mult,
+            )
+
+        def quant(j):
+            n = GROUPS[j][1]
+            co = work.tile([P, NG * n * P], U32, name="codes", align_bytes=64)
+            sc = work.tile([P, NG * n * P], U8, name="scales", align_bytes=64)
+            nc.vector.quantize_mx(out=co[:].bitcast(FP8X4), scales=sc[:], in_=x1[j][:].rearrange("p g m -> p (g m)"))
+            codes[j] = (co, sc)
+
+        def mx(j, v):
+            w = GROUPS[j][1] * P
+            t = (ps_m.tile([P, w], F32, name="mx") if j < NQ - 1 else ps_a.tile([P, w], F32, name="aT"))
+            co, sc = codes[j]
+            for g in range(NG):
+                gate_cols = slice(g * G + v * P, g * G + v * P + P)
+                token_cols = slice(g * w, g * w + w)
+                nc.tensor.matmul_mx(
+                    out=t[:],
+                    lhsT=w_codes[:, gate_cols].bitcast(FP8X4),
+                    lhsT_scale=w_scales[:, gate_cols],
+                    rhs=co[:, token_cols].bitcast(FP8X4),
+                    rhs_scale=sc[:, token_cols],
+                    start=(g == 0),
+                    stop=(g == NG - 1),
+                )
+            mx_ps[(j, v)] = t
+
+        def pre_out(j, v, engine):
+            t = work.tile([P, GROUPS[j][1] * P], F32, name="pre%d" % v)
+            if engine == "S":
+                nc.scalar.activation(out=t[:], in_=mx_ps[(j, v)][:], func=ACT.Identity, bias=b_col[:, v : v + 1], scale=2.0)
+            else:
+                nc.vector.tensor_scalar(
+                    out=t[:], in0=mx_ps[(j, v)][:], scalar1=2.0, scalar2=b_col[:, v : v + 1], op0=ALU.mult, op1=ALU.add
+                )
+            pre_t[(j, v)] = t
+
+        def pre_sum(j, v):
+            first, n = GROUPS[j]
+            t = (ps_s.tile([P, n, P], F32, name="sum") if j < NQ - 1 else ps_x.tile([P, n, P], F32, name="xT"))
+            for k in range(n):
+                nc.tensor.matmul(
+                    t[:, k, :], lhsT=h_t[first + k], rhs=u_sb[:, P * v : P * v + P], start=(k == 0), stop=False
+                )
+            for k in range(n):
+                nc.tensor.matmul(
+                    t[:, k, :],
+                    lhsT=pre_t[(j, v)][:, P * k : P * k + P],
+                    rhs=ident_f[:],
+                    is_transpose=True,
+                    start=False,
+                    stop=(k == n - 1),
+                )
+            pre_ps[(j, v)] = t
+
+        def gate(j, v):
+            t = keep.tile([P, GROUPS[j][1], H], F32, name="gate%d_%d" % (v, j))
+            nc.scalar.activation(out=t[:], in_=pre_ps[(j, v)][:], func=ACT.Tanh if v == G_HALF else ACT.Sigmoid)
+            gates[(j, v)] = t
+
+        def finish(j, engine):
+            first, n = GROUPS[j]
+            gi, gg = gates[(j, I_HALF)], gates[(j, G_HALF)]
+            ct, k = c_in[first]
+            cc = ct[:, k : k + n, :]
+            t = work.tile([P, n, H], F32, name="o")
+            parts = [slice(m, m + 2) for m in range(0, n, 2)]
+            for m in parts:
+                engine.tensor_tensor(out=gg[:, m, :], in0=gg[:, m, :], in1=cc[:, m, :], op=ALU.subtract)
+            for m in parts:
+                engine.tensor_tensor(out=gi[:, m, :], in0=gi[:, m, :], in1=gg[:, m, :], op=ALU.mult)
+            for m in parts:
+                engine.tensor_tensor(out=t[:, m, :], in0=gi[:, m, :], in1=cc[:, m, :], op=ALU.add)
+            nc.sync.dma_start(out=ov[:, first : first + n, :], in_=t[:])
+
+        def widen(g):
+            for m in range(PACK):
+                nc.vector.tensor_scalar(
+                    out=w_wide[:, g, m, :],
+                    in0=w_raw[:, g, m, :].bitcast(FP8),
+                    scalar1=w_sc[:, g, m : m + 1],
+                    scalar2=None,
+                    op0=ALU.mult,
+                )
+            nc.vector.tensor_copy(out=w_grp[:, g, :, :], in_=w_wide[:, g, :, :].rearrange("p m n -> p n m"))
+
+        def quant_w():
+            nc.vector.quantize_mx(
+                out=w_codes[:].bitcast(FP8X4),
+                scales=w_scales[:],
+                in_=w_grp[:].rearrange("p g n m -> p (g n m)"),
+            )
+
+        def bias():
+            t = ps_x.tile([P, P], BF16, name="xT")
+            nc.tensor.transpose(t[:], b_row[:], ident_b[:])
+            nc.vector.tensor_copy(out=b_col[:], in_=t[:, 0:2])
+
+        def quad(step, i, *args):
+            if 0 <= i < NQ:
+                step(i, *args)
+
+        def group(step, j, *args):
+            if 0 <= j < NQ - 1:
+                step(j, *args)
 
         nc.vector.memset(warm[:], 0.0)
         nc.scalar.activation(out=warm[:], in_=warm[:], func=ACT.Sigmoid)
         make_identity(nc, ident_b[:])
         make_identity(nc, ident_f[:])
-        load_hc(0, 1)
+        nc.vector.memset(b_row[:], 0.0)
+        load_h(0, 2)
         nc.sync.dma_start(out=q_raw[:], in_=q)
-        nc.sync.dma_start(out=w_raw[:], in_=w_bytes.rearrange("(g p t) n -> p g t n", p=P, t=PACK))
-        load_x(0)
-        nc.sync.dma_start(out=u_sb[:], in_=u)
-        nc.vector.memset(brow[:], 0.0)
-        nc.vector.memset(ones[:], 1.0)
-        nc.sync.dma_start(out=brow[0:1, :], in_=b.rearrange("(o n) -> o n", o=1))
-        nc.sync.dma_start(out=w_sc[:], in_=w_scale.rearrange("(g p t) o -> p g (t o)", p=P, t=PACK))
+        load_x(0, 2)
+        nc.sync.dma_start(out=w_raw[:], in_=w_bytes.rearrange("(g p m) n -> p g m n", p=P, m=PACK))
+        nc.sync.dma_start(out=w_sc[:], in_=w_scale.rearrange("(g p m) o -> p g (m o)", p=P, m=PACK))
         load_x(1)
-        load_hc(1, 4)
+        nc.sync.dma_start(out=b_row[0:2, :], in_=b.rearrange("(o n) -> o n", o=2))
+        nc.sync.dma_start(out=u_sb[:], in_=u)
         load_x(2)
-        load_c(0, 4)
+        load_h(2, 5)
         load_x(3)
+        load_c(0, 2)
 
-        ht = {}
-        st = {}
-        x1s = {}
-        cod = {}
-        pre = {}
-        hub = {}
-        gates_in = {}
-        outs = {}
-
-        def pe_h(k):
-            t, o = hs[k]
-            hp = ps_h.tile([P, 4, P], BF16, name="hp")
-            for j in range(4):
-                nc.tensor.transpose(hp[:, j, :], t[:, o + j, :], ident_b[:])
-            ht[k] = [hp, None]
-
-        def copy_h(k):
-            s = work.tile([P, 4, P], BF16, name="hT")
-            nc.scalar.copy(out=s[:], in_=ht[k][0][:])
-            ht[k][1] = s
-
-        def hT(i, jj):
-            return ht[i // 2][1][:, 2 * (i % 2) + jj, :]
-
-        def pe_a(i, g, jj):
-            a = ps_a.tile([P, PACK, P], F32, name="aT")
-            for t in range(PACK):
-                nc.tensor.matmul(a[:, t, :], lhsT=q_sb[:, g, t, :], rhs=hT(i, jj), start=True, stop=True)
-            st[(i, g, jj)] = a
-
-        def pe_x(i, g):
-            xp = ps_x.tile([P, 2 * P, 2], F32, name="xT")
-            words = xs[i][:].bitcast(F32)
-            for jj in range(2):
-                for v in range(2):
-                    nc.tensor.transpose(
-                        xp[:, P * jj : P * jj + P, v],
-                        words[:, jj, 256 * g + v : 256 * g + 256 : 2],
-                        ident_f[:],
-                    )
-            st[("x", i, g)] = xp
-
-        def pe_hu(i):
-            hp = ps_u.tile([P, 2, G], F32, name="hu")
-            for jj in range(2):
-                nc.tensor.matmul(hp[:, jj, :], lhsT=hT(i, jj), rhs=u_sb[:], start=True, stop=False)
-                nc.tensor.matmul(hp[:, jj, :], lhsT=ones[:], rhs=brow[:], start=False, stop=True)
-            hub[i] = hp
-
-        def pe_mx(i):
-            pt = ps_p.tile([P, 2, G], F32, name="pre")
-            co, sc = cod[i]
-            for jj in range(2):
-                if MIX:
-                    nc.tensor.matmul(pt[:, jj, :], lhsT=hT(i, jj), rhs=u_sb[:], start=True, stop=False)
-                for g in range(NG):
-                    cols = slice(g * 256 + jj * P, g * 256 + jj * P + P)
-                    nc.tensor.matmul_mx(
-                        out=pt[:, jj, :],
-                        lhsT=co[:, cols].bitcast(FP8X4),
-                        lhsT_scale=sc[:, cols],
-                        rhs=w_codes[:, g * G : g * G + G].bitcast(FP8X4),
-                        rhs_scale=w_scales[:, g * G : g * G + G],
-                        start=(g == 0 and not MIX),
-                        stop=(g == NG - 1 and not MIX),
-                    )
-                if MIX:
-                    nc.tensor.matmul(pt[:, jj, :], lhsT=ones[:], rhs=brow[:], start=False, stop=True)
-            pre[i] = pt
-
-        def act_sig(i, g, jj):
-            if jj == 0:
-                st[("s", i, g)] = work.tile([P, 2, P, PACK], F32, name="sg")
-            s = st[("s", i, g)]
-            nc.scalar.activation(
-                out=s[:, jj, :, :], in_=st[(i, g, jj)][:].rearrange("p t n -> p n t"), func=ACT.Sigmoid
-            )
-
-        def act_hu(i):
-            s = work.tile([P, 2, G], F32, name="hub")
-            nc.scalar.copy(out=s[:], in_=hub[i][:])
-            hub[i] = s
-
-        def act_gates(i):
-            src = pre[i] if MIX else gates_in[i]
-            gi = work.tile([P, 2, H], F32, name="gi")
-            gg = work.tile([P, 2, H], F32, name="gg")
-            nc.scalar.activation(out=gg[:], in_=src[:, :, H:G], func=ACT.Tanh)
-            nc.scalar.activation(out=gi[:], in_=src[:, :, 0:H], func=ACT.Sigmoid)
-            outs[i] = (gi, gg)
-
-        def dve_mult(i, g):
-            if g == 0:
-                x1s[i] = work.tile([P, NG, 1024], BF16, name="x1", align_bytes=64)
-            nc.vector.scalar_tensor_tensor(
-                out=x1s[i][:, g, :],
-                in0=st[("x", i, g)][:].rearrange("p n v -> p (n v)").bitcast(BF16),
-                scalar=2.0,
-                in1=st[("s", i, g)][:].rearrange("p j n t -> p (j n t)"),
-                op0=ALU.mult,
-                op1=ALU.mult,
-            )
-
-        def dve_quant(i):
-            co = work.tile([P, 512], U32, name="codes", align_bytes=64)
-            sc = work.tile([P, 512], U8, name="scales", align_bytes=64)
-            nc.vector.quantize_mx(
-                out=co[:].bitcast(FP8X4), scales=sc[:], in_=x1s[i][:].rearrange("p g m -> p (g m)")
-            )
-            cod[i] = (co, sc)
-
-        def dve_add(i):
-            s = work.tile([P, 2, G], F32, name="pre_sb")
-            nc.vector.tensor_tensor(out=s[:], in0=pre[i][:], in1=hub[i][:], op=ALU.add)
-            gates_in[i] = s
-
-        def fin(i):
-            gi, gg = outs[i]
-            t, o = cs[i]
-            cc = t[:, o : o + 2, :]
-            ob = work.tile([P, 2, H], F32, name="ob")
-            e = nc.vector if i == NP - 1 else nc.gpsimd
-            e.tensor_tensor(out=gg[:], in0=gg[:], in1=cc, op=ALU.subtract)
-            e.tensor_tensor(out=gi[:], in0=gi[:], in1=gg[:], op=ALU.mult)
-            e.tensor_tensor(out=ob[:], in0=gi[:], in1=cc, op=ALU.add)
-            nc.sync.dma_start(out=ov[:, 2 * i : 2 * i + 2, :], in_=ob[:])
-
+        V, S = nc.vector, nc.scalar
         with tc.manual_schedule():
-            pe_h(0)
-            copy_h(0)
-            qv = q_raw[:].rearrange("k (g p t) -> k g t p", p=P, t=PACK)
-            nc.vector.tensor_copy(out=q_sb[:, 0, :, :], in_=qv[:, 0, :, :])
-            nc.vector.tensor_copy(out=q_sb[:, 1, :, :], in_=qv[:, 1, :, :])
-            for t in range(PACK):
-                nc.vector.tensor_scalar(
-                    out=w_wide[:, 0, t, :],
-                    in0=w_raw[:, 0, t, :].bitcast(FP8),
-                    scalar1=w_sc[:, 0, t : t + 1],
-                    scalar2=None,
-                    op0=ALU.mult,
-                )
-            nc.vector.tensor_copy(out=w_grp[:, 0, :, :], in_=w_wide[:, 0, :, :].rearrange("p t n -> p n t"))
-            nc.gpsimd.tensor_copy(out=w_f32[:], in_=w_raw[:, 1, :, :].bitcast(FP8))
-            for t in range(PACK):
-                nc.gpsimd.tensor_scalar(
-                    out=w_wide[:, 1, t, :],
-                    in0=w_f32[:, t, :],
-                    scalar1=w_sc[:, 1, t : t + 1],
-                    scalar2=0.0,
-                    op0=ALU.mult,
-                    op1=ALU.add,
-                )
-            nc.gpsimd.tensor_scalar(
-                out=w_grp[:, 1, :, :],
-                in0=w_wide[:, 1, :, :].rearrange("p t n -> p n t"),
-                scalar1=1.0,
-                scalar2=0.0,
-                op0=ALU.mult,
-                op1=ALU.add,
-            )
-            for i in range(NP + 4):
-                if i + 4 < NP:
-                    load_x(i + 4)
-                    if i == 2:
-                        load_hc(4, 10)
-                    if i == 4:
-                        load_c(4, 16)
-                    if i == 8:
-                        load_hc(10, 16)
-                    if i == 10:
-                        load_c(16, 32)
-                if i < NP:
-                    pe_a(i, 0, 0)
-                    pe_x(i, 0)
-                    pe_a(i, 0, 1)
-                    if not MIX:
-                        pe_hu(i)
-                    pe_a(i, 1, 0)
-                    pe_x(i, 1)
-                    pe_a(i, 1, 1)
-                if i % 2 == 0 and i // 2 + 1 < NP // 2:
-                    pe_h(i // 2 + 1)
-                if 0 <= i - 2 < NP:
-                    pe_mx(i - 2)
-                if i < NP:
-                    act_sig(i, 0, 0)
-                    act_sig(i, 0, 1)
-                    if not MIX:
-                        act_hu(i)
-                    act_sig(i, 1, 0)
-                    act_sig(i, 1, 1)
-                if 0 <= i - 3 < NP:
-                    act_gates(i - 3)
-                if i < NP:
-                    dve_mult(i, 0)
-                if 0 <= i - 1 < NP:
-                    dve_quant(i - 1)
-                if i % 2 == 0 and i // 2 + 1 < NP // 2:
-                    copy_h(i // 2 + 1)
-                if i < NP:
-                    dve_mult(i, 1)
-                if i == 1:
-                    nc.vector.quantize_mx(
-                        out=w_codes[:].bitcast(FP8X4),
-                        scales=w_scales[:],
-                        in_=w_grp[:].rearrange("p g n t -> p (g n t)"),
-                    )
-                if not MIX and 0 <= i - 2 < NP:
-                    dve_add(i - 2)
-                if 0 <= i - 3 < NP:
-                    fin(i - 3)
+            h_turn(0)
+            h_copy(0, V.tensor_copy)
+            q_view = q_raw[:].rearrange("k (g p m) -> k g m p", p=P, m=PACK)
+            for g in range(NG):
+                V.tensor_copy(out=q_sb[:, g, :, :], in_=q_view[:, g, :, :])
+            for n in range(NQ + 2):
+                for j in (2 * n + 4, 2 * n + 5):
+                    if j < 2 * NQ:
+                        load_x(j)
+                if n == 1:
+                    load_h(5, 10)
+                    load_c(2, 8)
+                if n == 4:
+                    load_h(10, 16)
+                    load_c(8, 16)
+                quad(a_mm, n, 0)
+                group(pre_sum, n - 2, 1)
+                group(gate, n - 2, 1)
+                quad(h_turn, n + 1)
+                quad(x_turn, n, 0)
+                quad(sig, n, 0)
+                quad(h_copy, n + 1, V.tensor_copy)
+                quad(a_mm, n, 1)
+                quad(a_mm, n, 2)
+                group(quant, n - 1)
+                group(pre_sum, n - 2, 0)
+                quad(sig, n, 1)
+                quad(sig, n, 2)
+                quad(x_turn, n, 1)
+                quad(mult, n, 0)
+                if n == 0:
+                    widen(0)
+                quad(x_turn, n, 2)
+                if n == 0:
+                    bias()
+                group(gate, n - 2, 0)
+                quad(a_mm, n, 3)
+                group(mx, n - 1, 1)
+                quad(sig, n, 3)
+                group(finish, n - 2, nc.gpsimd)
+                quad(a_mm, n, 4)
+                group(pre_out, n - 1, 1, "V")
+                quad(a_mm, n, 5)
+                quad(sig, n, 4)
+                quad(x_turn, n, 3)
+                quad(mult, n, 1)
+                if n == 0:
+                    widen(1)
+                if n == NQ - 1:
+                    quant(NQ - 1)
+                quad(sig, n, 5)
+                quad(a_mm, n, 6)
+                quad(a_mm, n, 7)
+                quad(sig, n, 6)
+                group(mx, n - 1, 0)
+                quad(mult, n, 2)
+                if n == 0:
+                    quant_w()
+                quad(sig, n, 7)
+                group(pre_out, n - 1, 0, "S")
+                quad(mult, n, 3)
+                if n == NQ - 1:
+                    quant(NQ)
+            mx(15, 1)
+            mx(15, 0)
+            pre_out(15, 1, "V")
+            pre_out(15, 0, "S")
+            mx(16, 1)
+            mx(16, 0)
+            pre_out(16, 1, "V")
+            pre_out(16, 0, "S")
+            pre_sum(15, 1)
+            pre_sum(15, 0)
+            gate(15, 1)
+            gate(15, 0)
+            finish(15, nc.gpsimd)
+            pre_sum(16, 1)
+            pre_sum(16, 0)
+            gate(16, 1)
+            gate(16, 0)
+            finish(16, V)

@@ -85,33 +85,34 @@ def tile_mogrifieroneroundcoupledlstmcell_t_kernel(tc, x, h, c, q, w_bytes, w_sc
         def h_copy(i, engine_copy):
             t = keep.tile([P, 4, P], BF16, name="ht%d" % i)
             engine_copy(out=t[:], in_=h_ps[i][:])
-            for j in range(4):
-                h_t[4 * i + j] = t[:, j, :]
+            h_t[i] = t
 
         def a_mm(i, k):
-            tile, g = 4 * i + 2 * (k // 4) + k % 2, k // 2 % 2
-            t = ps_a.tile([P, PACK, P], F32, name="aT")
-            for m in range(PACK):
-                nc.tensor.matmul(t[:, m, :], lhsT=q_sb[:, g, m, :], rhs=h_t[tile], start=True, stop=True)
+            pair, g, m = k // 4, k // 2 % 2, k % 2
+            if m == 0:
+                x_ps[(i, k // 2)] = ps_x.tile([P, 2, 2 * P], F32, name="xT")
+            xt = x_ps[(i, k // 2)]
+            words = x_in[2 * i + pair][:].bitcast(F32)
+            t = ps_a.tile([P, 2, 2 * P], F32, name="aT")
+            for e in range(2):
+                nc.tensor.transpose(
+                    xt[:, e, P * m : P * m + P], words[:, m, 256 * g + e : 256 * g + 256 : 2], ident_f[:]
+                )
+                nc.tensor.matmul(
+                    t[:, e, :],
+                    lhsT=q_sb[:, g, 2 * m + e, :],
+                    rhs=h_t[i][:, 2 * pair : 2 * pair + 2, :].rearrange("p j n -> p (j n)"),
+                    start=True,
+                    stop=True,
+                )
             a_ps[(i, k)] = t
-
-        def x_turn(i, k):
-            pair, g = 2 * i + k // 2, k % 2
-            t = ps_x.tile([P, 2, 2 * P], F32, name="xT")
-            words = x_in[pair][:].bitcast(F32)
-            for j in range(2):
-                for m in range(2):
-                    nc.tensor.transpose(
-                        t[:, m, P * j : P * j + P], words[:, j, 256 * g + m : 256 * g + 256 : 2], ident_f[:]
-                    )
-            x_ps[(i, k)] = t
 
         def sig(i, k):
             if k % 2 == 0:
-                sg[(i, k // 2)] = sgp.tile([P, 2, P, PACK], F32, name="sg")
+                sg[(i, k // 2)] = sgp.tile([P, 2, 2 * P, 2], F32, name="sg")
             nc.scalar.activation(
                 out=sg[(i, k // 2)][:, k % 2, :, :],
-                in_=a_ps[(i, k)][:].rearrange("p m n -> p n m"),
+                in_=a_ps[(i, k)][:].rearrange("p e n -> p n e"),
                 func=ACT.Sigmoid,
             )
 
@@ -123,7 +124,7 @@ def tile_mogrifieroneroundcoupledlstmcell_t_kernel(tc, x, h, c, q, w_bytes, w_sc
             nc.vector.tensor_tensor(
                 out=x1[j][:, g, 1024 * slot : 1024 * slot + 1024].rearrange("p (n m e) -> p n m e", m=2, e=2),
                 in0=x_ps[(i, k)][:].bitcast(BF16).rearrange("p m (n e) -> p n m e", e=2),
-                in1=sg[(i, k)][:].rearrange("p j n (m e) -> p (j n) m e", m=2),
+                in1=sg[(i, k)][:].rearrange("p m n e -> p n m e"),
                 op=ALU.mult,
             )
 
@@ -167,7 +168,7 @@ def tile_mogrifieroneroundcoupledlstmcell_t_kernel(tc, x, h, c, q, w_bytes, w_sc
             t = (ps_s.tile([P, n, P], F32, name="sum") if j < NQ - 1 else ps_x.tile([P, n, P], F32, name="xT"))
             for k in range(n):
                 nc.tensor.matmul(
-                    t[:, k, :], lhsT=h_t[first + k], rhs=u_sb[:, P * v : P * v + P], start=(k == 0), stop=False
+                    t[:, k, :], lhsT=h_t[(first + k) // 4][:, (first + k) % 4, :], rhs=u_sb[:, P * v : P * v + P], start=(k == 0), stop=False
                 )
             for k in range(n):
                 nc.tensor.matmul(
@@ -266,43 +267,39 @@ def tile_mogrifieroneroundcoupledlstmcell_t_kernel(tc, x, h, c, q, w_bytes, w_sc
                 if n == 4:
                     load_h(10, 16)
                     load_c(8, 16)
-                quad(a_mm, n, 0)
                 group(pre_sum, n - 2, 1)
-                group(gate, n - 2, 1)
                 quad(h_turn, n + 1)
-                quad(x_turn, n, 0)
+                quad(a_mm, n, 0)
+                group(gate, n - 2, 1)
+                quad(a_mm, n, 1)
                 quad(sig, n, 0)
                 quad(h_copy, n + 1, V.tensor_copy)
-                quad(a_mm, n, 1)
-                quad(a_mm, n, 2)
-                group(quant, n - 1)
                 group(pre_sum, n - 2, 0)
+                group(quant, n - 1)
                 quad(sig, n, 1)
-                quad(sig, n, 2)
-                quad(x_turn, n, 1)
+                quad(a_mm, n, 2)
+                group(gate, n - 2, 0)
+                quad(a_mm, n, 3)
                 quad(mult, n, 0)
                 if n == 0:
                     widen(0)
-                quad(x_turn, n, 2)
-                if n == 0:
-                    bias()
-                group(gate, n - 2, 0)
-                quad(a_mm, n, 3)
+                quad(sig, n, 2)
                 group(mx, n - 1, 1)
-                quad(sig, n, 3)
                 group(finish, n - 2, nc.gpsimd)
+                quad(sig, n, 3)
                 quad(a_mm, n, 4)
                 group(pre_out, n - 1, 1, "V")
                 quad(a_mm, n, 5)
+                if n == 0:
+                    bias()
                 quad(sig, n, 4)
-                quad(x_turn, n, 3)
                 quad(mult, n, 1)
                 if n == 0:
                     widen(1)
                 if n == NQ - 1:
                     quant(NQ - 1)
-                quad(sig, n, 5)
                 quad(a_mm, n, 6)
+                quad(sig, n, 5)
                 quad(a_mm, n, 7)
                 quad(sig, n, 6)
                 group(mx, n - 1, 0)

@@ -14,318 +14,388 @@ ALU = mybir.AluOpType
 
 P = 128
 N, D, H = 8192, 1024, 128
-G = 2 * H
-NT = N // P
-NQ = NT // 4
+GATES = 2 * H
+TILES = N // P
+QUADS = TILES // 4
 PACK = 4
-NG = D // (P * PACK)
-FLOPS = 2 * N * (H * D + H * G + D * G)
-GROUPS = [(4 * i, 4) for i in range(NQ - 1)] + [(NT - 4, 2), (NT - 2, 2)]
+K_PASS = P * PACK
+PASSES = D // K_PASS
+FLOPS = 2 * N * (H * D + H * GATES + D * GATES)
+
+GROUPS = [(4 * i, 4) for i in range(QUADS - 1)] + [(TILES - 4, 2), (TILES - 2, 2)]
+LAST_QUAD = QUADS - 1
+PAIR_A, PAIR_B = QUADS - 1, QUADS
+
 I_HALF, G_HALF = 0, 1
 
 
 def tile_mogrifieroneroundcoupledlstmcell_t_kernel(tc, x, h, c, q, w_bytes, w_scale, u, b, out):
     nc = tc.nc
-    xv = x.rearrange("(p j) d -> p j d", p=P)
-    hv = h.rearrange("(p j) d -> p j d", p=P)
-    cv = c.rearrange("(p j) d -> p j d", p=P)
-    ov = out.rearrange("(p j) d -> p j d", p=P)
+    V, S = nc.vector, nc.scalar
+    x_hbm = x.rearrange("(p j) d -> p j d", p=P)
+    h_hbm = h.rearrange("(p j) d -> p j d", p=P)
+    c_hbm = c.rearrange("(p j) d -> p j d", p=P)
+    out_hbm = out.rearrange("(p j) d -> p j d", p=P)
+
     with ExitStack() as ctx:
         keep = ctx.enter_context(tc.tile_pool(name="keep", bufs=1))
-        xin = ctx.enter_context(tc.tile_pool(name="xin", bufs=6))
+        x_pool = ctx.enter_context(tc.tile_pool(name="x_pool", bufs=6))
         work = ctx.enter_context(tc.tile_pool(name="work", bufs=3))
-        sgp = ctx.enter_context(tc.tile_pool(name="sgp", bufs=4))
-        ps_a = ctx.enter_context(tc.psum_pool(name="ps_a", bufs=3))
-        ps_x = ctx.enter_context(tc.psum_pool(name="ps_x", bufs=3))
-        ps_m = ctx.enter_context(tc.psum_pool(name="ps_m", bufs=1))
-        ps_s = ctx.enter_context(tc.psum_pool(name="ps_s", bufs=1))
+        sig_pool = ctx.enter_context(tc.tile_pool(name="sig_pool", bufs=4))
+        banks = {
+            "a": ctx.enter_context(tc.psum_pool(name="psum_a", bufs=3)),
+            "turn": ctx.enter_context(tc.psum_pool(name="psum_turn", bufs=3)),
+            "mx": ctx.enter_context(tc.psum_pool(name="psum_mx", bufs=1)),
+            "pre": ctx.enter_context(tc.psum_pool(name="psum_pre", bufs=1)),
+        }
 
-        ident_f = keep.tile([P, P], F32, name="ident_f")
-        ident_b = keep.tile([P, P], BF16, name="ident_b")
-        b_row = keep.tile([P, P], BF16, name="b_row")
-        b_col = keep.tile([P, 2], F32, name="b_col")
+        ident_f32 = keep.tile([P, P], F32, name="ident_f32")
+        ident_bf16 = keep.tile([P, P], BF16, name="ident_bf16")
+        b_rows = keep.tile([P, P], BF16, name="b_rows")
+        b_cols = keep.tile([P, 2], F32, name="b_cols")
         q_raw = keep.tile([P, D], BF16, name="q_raw")
-        q_sb = keep.tile([P, NG, PACK, P], BF16, name="q_sb")
-        u_sb = keep.tile([P, G], BF16, name="u_sb")
-        w_raw = keep.tile([P, NG, PACK, G], U8, name="w_raw", align_bytes=64)
-        w_sc = keep.tile([P, NG, PACK], F32, name="w_sc")
-        w_wide = keep.tile([P, NG, PACK, G], BF16, name="w_wide")
-        w_grp = keep.tile([P, NG, G, PACK], BF16, name="w_grp", align_bytes=64)
-        w_codes = keep.tile([P, NG * G], U32, name="w_codes", align_bytes=64)
-        w_scales = keep.tile([P, NG * G], U8, name="w_scales", align_bytes=64)
-        warm = keep.tile([P, 1], F32, name="warm")
+        q_sb = keep.tile([P, PASSES, PACK, P], BF16, name="q_sb")
+        u_sb = keep.tile([P, GATES], BF16, name="u_sb")
+        w_codes_in = keep.tile([P, PASSES, PACK, GATES], U8, name="w_codes_in", align_bytes=64)
+        w_scale_in = keep.tile([P, PASSES, PACK], F32, name="w_scale_in")
+        w_wide = keep.tile([P, PASSES, PACK, GATES], BF16, name="w_wide")
+        w_grouped = keep.tile([P, PASSES, GATES, PACK], BF16, name="w_grouped", align_bytes=64)
+        w_mx = keep.tile([P, PASSES * GATES], U32, name="w_mx", align_bytes=64)
+        w_mx_scale = keep.tile([P, PASSES * GATES], U8, name="w_mx_scale", align_bytes=64)
+        table_seed = keep.tile([P, 1], F32, name="table_seed")
 
-        h_in, c_in, x_in, h_ps, h_t, a_ps, x_ps, sg, x1, codes, mx_ps, pre_t, pre_ps, gates = ({} for k in range(14))
+        x_in, h_in, c_in, h_psum, h_t, a_psum, x_psum, sig_a = {}, {}, {}, {}, {}, {}, {}, {}
+        x1, x1_mx, mx_psum, mx_t, pre_psum, gates, result = {}, {}, {}, {}, {}, {}, {}
 
         def load_h(lo, hi):
             t = keep.tile([P, (hi - lo) * 4, H], BF16, name="h%d" % lo)
-            nc.sync.dma_start(out=t[:], in_=hv[:, 4 * lo : 4 * hi, :])
+            nc.sync.dma_start(out=t[:], in_=h_hbm[:, 4 * lo : 4 * hi, :])
             for i in range(lo, hi):
                 h_in[i] = t[:, 4 * (i - lo) : 4 * (i - lo) + 4, :]
 
         def load_c(lo, hi):
             t = keep.tile([P, (hi - lo) * 4, H], BF16, name="c%d" % lo)
-            nc.sync.dma_start(out=t[:], in_=cv[:, 4 * lo : 4 * hi, :])
-            for i in range(4 * lo, 4 * hi):
-                c_in[i] = (t, i - 4 * lo)
+            nc.sync.dma_start(out=t[:], in_=c_hbm[:, 4 * lo : 4 * hi, :])
+            for j in range(4 * lo, 4 * hi, 2):
+                c_in[j] = (t, j - 4 * lo)
 
-        def load_x(i, pieces=1):
-            t = xin.tile([P, 2, D], BF16, name="x_in")
-            w = 2 // pieces
-            for k in range(0, 2, w):
-                nc.sync.dma_start(out=t[:, k : k + w, :], in_=xv[:, 2 * i + k : 2 * i + k + w, :])
-            x_in[i] = t
+        def load_x(pair):
+            t = x_pool.tile([P, 2, D], BF16, name="x")
+            nc.sync.dma_start(out=t[:], in_=x_hbm[:, 2 * pair : 2 * pair + 2, :])
+            x_in[pair] = t
 
-        def h_turn(i):
-            t = ps_x.tile([P, 4, P], BF16, name="xT")
-            for j in range(4):
-                nc.tensor.transpose(t[:, j, :], h_in[i][:, j, :], ident_b[:])
-            h_ps[i] = t
+        def h_turn(lo, n, bank):
+            t = banks[bank].tile([P, 4 * n, P], BF16, name=bank)
+            for i in range(n):
+                for j in range(4):
+                    nc.tensor.transpose(t[:, 4 * i + j, :], h_in[lo + i][:, j, :], ident_bf16[:])
+            h_psum[lo] = t
 
-        def h_copy(i, engine_copy):
-            t = keep.tile([P, 4, P], BF16, name="ht%d" % i)
-            engine_copy(out=t[:], in_=h_ps[i][:])
-            h_t[i] = t
+        def h_copy(lo, n, copy):
+            t = keep.tile([P, 4 * n, P], BF16, name="ht%d" % lo)
+            copy(out=t[:], in_=h_psum[lo][:])
+            for i in range(n):
+                h_t[lo + i] = t[:, 4 * i : 4 * i + 4, :]
 
-        def a_mm(i, k):
-            pair, g, m = k // 4, k // 2 % 2, k % 2
+        def a_and_x(i, k):
+            pair, s, m = k // 4, k // 2 % 2, k % 2
             if m == 0:
-                x_ps[(i, k // 2)] = ps_x.tile([P, 2, 2 * P], F32, name="xT")
-            xt = x_ps[(i, k // 2)]
+                x_psum[(i, k // 2)] = banks["turn"].tile([P, 2, 2 * P], F32, name="turn")
+            turned = x_psum[(i, k // 2)]
             words = x_in[2 * i + pair][:].bitcast(F32)
-            t = ps_a.tile([P, 2, 2 * P], F32, name="aT")
+            t = banks["a"].tile([P, 2, 2 * P], F32, name="a")
             for e in range(2):
                 nc.tensor.transpose(
-                    xt[:, e, P * m : P * m + P], words[:, m, 256 * g + e : 256 * g + 256 : 2], ident_f[:]
+                    turned[:, e, P * m : P * m + P],
+                    words[:, m, 256 * s + e : 256 * s + 256 : 2],
+                    ident_f32[:],
                 )
                 nc.tensor.matmul(
                     t[:, e, :],
-                    lhsT=q_sb[:, g, 2 * m + e, :],
+                    lhsT=q_sb[:, s, 2 * m + e, :],
                     rhs=h_t[i][:, 2 * pair : 2 * pair + 2, :].rearrange("p j n -> p (j n)"),
                     start=True,
                     stop=True,
                 )
-            a_ps[(i, k)] = t
+            a_psum[(i, k)] = t
 
-        def sig(i, k):
+        def sigmoid_a(i, k):
             if k % 2 == 0:
-                sg[(i, k // 2)] = sgp.tile([P, 2, 2 * P, 2], F32, name="sg")
-            nc.scalar.activation(
-                out=sg[(i, k // 2)][:, k % 2, :, :],
-                in_=a_ps[(i, k)][:].rearrange("p e n -> p n e"),
+                sig_a[(i, k // 2)] = sig_pool.tile([P, 2, 2 * P, 2], F32, name="sig")
+            S.activation(
+                out=sig_a[(i, k // 2)][:, k % 2, :, :],
+                in_=a_psum[(i, k)][:].rearrange("p e n -> p n e"),
                 func=ACT.Sigmoid,
             )
 
-        def mult(i, k):
-            pair, g = k // 2, k % 2
-            j, slot = (i, pair) if i < NQ - 1 else (NQ - 1 + pair, 0)
+        def gate_x(i, k):
+            pair, s = k // 2, k % 2
+            j, place = (i, pair) if i < LAST_QUAD else (PAIR_A + pair, 0)
             if j not in x1:
-                x1[j] = work.tile([P, NG, GROUPS[j][1] * 512], BF16, name="x1", align_bytes=64)
-            nc.vector.tensor_tensor(
-                out=x1[j][:, g, 1024 * slot : 1024 * slot + 1024].rearrange("p (n m e) -> p n m e", m=2, e=2),
-                in0=x_ps[(i, k)][:].bitcast(BF16).rearrange("p m (n e) -> p n m e", e=2),
-                in1=sg[(i, k)][:].rearrange("p m n e -> p n m e"),
+                x1[j] = work.tile([P, PASSES, GROUPS[j][1] * K_PASS], BF16, name="x1", align_bytes=64)
+            V.tensor_tensor(
+                out=x1[j][:, s, 1024 * place : 1024 * place + 1024].rearrange("p (n m e) -> p n m e", m=2, e=2),
+                in0=x_psum[(i, k)][:].bitcast(BF16).rearrange("p m (n e) -> p n m e", e=2),
+                in1=sig_a[(i, k)][:].rearrange("p m n e -> p n m e"),
                 op=ALU.mult,
             )
 
-        def quant(j):
-            n = GROUPS[j][1]
-            co = work.tile([P, NG * n * P], U32, name="codes", align_bytes=64)
-            sc = work.tile([P, NG * n * P], U8, name="scales", align_bytes=64)
-            nc.vector.quantize_mx(out=co[:].bitcast(FP8X4), scales=sc[:], in_=x1[j][:].rearrange("p g m -> p (g m)"))
-            codes[j] = (co, sc)
+        def quantize_x1(j):
+            words = PASSES * GROUPS[j][1] * P
+            codes = work.tile([P, words], U32, name="x1_mx", align_bytes=64)
+            scales = work.tile([P, words], U8, name="x1_mx_scale", align_bytes=64)
+            V.quantize_mx(
+                out=codes[:].bitcast(FP8X4), scales=scales[:], in_=x1[j][:].rearrange("p s m -> p (s m)")
+            )
+            x1_mx[j] = (codes, scales)
 
-        def mx(j, v):
-            w = GROUPS[j][1] * P
-            t = (ps_m.tile([P, w], F32, name="mx") if j < NQ - 1 else ps_a.tile([P, w], F32, name="aT"))
-            co, sc = codes[j]
-            for g in range(NG):
-                gate_cols = slice(g * G + v * P, g * G + v * P + P)
-                token_cols = slice(g * w, g * w + w)
+        def mx_product(j, half, bank="mx"):
+            tokens = GROUPS[j][1] * P
+            t = banks[bank].tile([P, tokens], F32, name=bank)
+            codes, scales = x1_mx[j]
+            for s in range(PASSES):
+                w_cols = slice(s * GATES + half * P, s * GATES + half * P + P)
+                x_cols = slice(s * tokens, s * tokens + tokens)
                 nc.tensor.matmul_mx(
                     out=t[:],
-                    lhsT=w_codes[:, gate_cols].bitcast(FP8X4),
-                    lhsT_scale=w_scales[:, gate_cols],
-                    rhs=co[:, token_cols].bitcast(FP8X4),
-                    rhs_scale=sc[:, token_cols],
-                    start=(g == 0),
-                    stop=(g == NG - 1),
+                    lhsT=w_mx[:, w_cols].bitcast(FP8X4),
+                    lhsT_scale=w_mx_scale[:, w_cols],
+                    rhs=codes[:, x_cols].bitcast(FP8X4),
+                    rhs_scale=scales[:, x_cols],
+                    start=(s == 0),
+                    stop=(s == PASSES - 1),
                 )
-            mx_ps[(j, v)] = t
+            mx_psum[(j, half)] = t
 
-        def pre_out(j, v, engine):
-            t = work.tile([P, GROUPS[j][1] * P], F32, name="pre%d" % v)
-            if engine == "S":
-                nc.scalar.activation(out=t[:], in_=mx_ps[(j, v)][:], func=ACT.Identity, bias=b_col[:, v : v + 1], scale=2.0)
+        def mx_copy(j, half, engine):
+            t = work.tile([P, GROUPS[j][1] * P], F32, name="mx_t%d" % half)
+            b_col = b_cols[:, half : half + 1]
+            if engine is S:
+                S.activation(out=t[:], in_=mx_psum[(j, half)][:], func=ACT.Identity, bias=b_col, scale=2.0)
             else:
-                nc.vector.tensor_scalar(
-                    out=t[:], in0=mx_ps[(j, v)][:], scalar1=2.0, scalar2=b_col[:, v : v + 1], op0=ALU.mult, op1=ALU.add
+                V.tensor_scalar(
+                    out=t[:], in0=mx_psum[(j, half)][:], scalar1=2.0, scalar2=b_col, op0=ALU.mult, op1=ALU.add
                 )
-            pre_t[(j, v)] = t
+            mx_t[(j, half)] = t
 
-        def pre_sum(j, v):
+        def add_h_u(j, half, bank="pre"):
             first, n = GROUPS[j]
-            t = (ps_s.tile([P, n, P], F32, name="sum") if j < NQ - 1 else ps_x.tile([P, n, P], F32, name="xT"))
+            t = banks[bank].tile([P, n, P], F32, name=bank)
             for k in range(n):
+                i, tile = (first + k) // 4, (first + k) % 4
                 nc.tensor.matmul(
-                    t[:, k, :], lhsT=h_t[(first + k) // 4][:, (first + k) % 4, :], rhs=u_sb[:, P * v : P * v + P], start=(k == 0), stop=False
+                    t[:, k, :],
+                    lhsT=h_t[i][:, tile, :],
+                    rhs=u_sb[:, P * half : P * half + P],
+                    start=(k == 0),
+                    stop=False,
                 )
             for k in range(n):
                 nc.tensor.matmul(
                     t[:, k, :],
-                    lhsT=pre_t[(j, v)][:, P * k : P * k + P],
-                    rhs=ident_f[:],
+                    lhsT=mx_t[(j, half)][:, P * k : P * k + P],
+                    rhs=ident_f32[:],
                     is_transpose=True,
                     start=False,
                     stop=(k == n - 1),
                 )
-            pre_ps[(j, v)] = t
+            pre_psum[(j, half)] = t
 
-        def gate(j, v):
-            t = keep.tile([P, GROUPS[j][1], H], F32, name="gate%d_%d" % (v, j))
-            nc.scalar.activation(out=t[:], in_=pre_ps[(j, v)][:], func=ACT.Tanh if v == G_HALF else ACT.Sigmoid)
-            gates[(j, v)] = t
+        def gate(j, half):
+            t = keep.tile([P, GROUPS[j][1], H], F32, name="gate%d_%d" % (half, j))
+            S.activation(out=t[:], in_=pre_psum[(j, half)][:], func=ACT.Tanh if half == G_HALF else ACT.Sigmoid)
+            gates[(j, half)] = t
 
-        def finish(j, engine):
+        def update(j, engine, steps=(0, 1, 2), tiles=2):
             first, n = GROUPS[j]
-            gi, gg = gates[(j, I_HALF)], gates[(j, G_HALF)]
-            ct, k = c_in[first]
-            cc = ct[:, k : k + n, :]
-            t = work.tile([P, n, H], F32, name="o")
-            parts = [slice(m, m + 2) for m in range(0, n, 2)]
-            for m in parts:
-                engine.tensor_tensor(out=gg[:, m, :], in0=gg[:, m, :], in1=cc[:, m, :], op=ALU.subtract)
-            for m in parts:
-                engine.tensor_tensor(out=gi[:, m, :], in0=gi[:, m, :], in1=gg[:, m, :], op=ALU.mult)
-            for m in parts:
-                engine.tensor_tensor(out=t[:, m, :], in0=gi[:, m, :], in1=cc[:, m, :], op=ALU.add)
-            nc.sync.dma_start(out=ov[:, first : first + n, :], in_=t[:])
+            i_t, g_t = gates[(j, I_HALF)], gates[(j, G_HALF)]
+            c_t, place = c_in[first]
+            if 0 in steps:
+                result[j] = work.tile([P, n, H], F32, name="result")
+            for step in steps:
+                for k in range(0, n, tiles):
+                    z = slice(k, k + tiles)
+                    c_z = c_t[:, place + k : place + k + tiles, :]
+                    if step == 0:
+                        engine.tensor_tensor(out=g_t[:, z, :], in0=g_t[:, z, :], in1=c_z, op=ALU.subtract)
+                    elif step == 1:
+                        engine.tensor_tensor(out=i_t[:, z, :], in0=i_t[:, z, :], in1=g_t[:, z, :], op=ALU.mult)
+                    else:
+                        engine.tensor_tensor(out=result[j][:, z, :], in0=i_t[:, z, :], in1=c_z, op=ALU.add)
+            if 2 in steps:
+                nc.sync.dma_start(out=out_hbm[:, first : first + n, :], in_=result[j][:])
 
-        def widen(g):
-            for m in range(PACK):
-                nc.vector.tensor_scalar(
-                    out=w_wide[:, g, m, :],
-                    in0=w_raw[:, g, m, :].bitcast(FP8),
-                    scalar1=w_sc[:, g, m : m + 1],
+        def widen_w(s):
+            for t in range(PACK):
+                V.tensor_scalar(
+                    out=w_wide[:, s, t, :],
+                    in0=w_codes_in[:, s, t, :].bitcast(FP8),
+                    scalar1=w_scale_in[:, s, t : t + 1],
                     scalar2=None,
                     op0=ALU.mult,
                 )
-            nc.vector.tensor_copy(out=w_grp[:, g, :, :], in_=w_wide[:, g, :, :].rearrange("p m n -> p n m"))
+            V.tensor_copy(out=w_grouped[:, s, :, :], in_=w_wide[:, s, :, :].rearrange("p t n -> p n t"))
 
-        def quant_w():
-            nc.vector.quantize_mx(
-                out=w_codes[:].bitcast(FP8X4),
-                scales=w_scales[:],
-                in_=w_grp[:].rearrange("p g n m -> p (g n m)"),
+        def quantize_w():
+            V.quantize_mx(
+                out=w_mx[:].bitcast(FP8X4),
+                scales=w_mx_scale[:],
+                in_=w_grouped[:].rearrange("p s n t -> p (s n t)"),
             )
 
-        def bias():
-            t = ps_x.tile([P, P], BF16, name="xT")
-            nc.tensor.transpose(t[:], b_row[:], ident_b[:])
-            nc.vector.tensor_copy(out=b_col[:], in_=t[:, 0:2])
+        def turn_b():
+            t = banks["turn"].tile([P, P], BF16, name="turn")
+            nc.tensor.transpose(t[:], b_rows[:], ident_bf16[:])
+            V.tensor_copy(out=b_cols[:], in_=t[:, 0:2])
 
         def quad(step, i, *args):
-            if 0 <= i < NQ:
+            if 0 <= i < QUADS:
                 step(i, *args)
 
         def group(step, j, *args):
-            if 0 <= j < NQ - 1:
+            if 0 <= j < LAST_QUAD:
                 step(j, *args)
 
-        nc.vector.memset(warm[:], 0.0)
-        nc.scalar.activation(out=warm[:], in_=warm[:], func=ACT.Sigmoid)
-        make_identity(nc, ident_b[:])
-        make_identity(nc, ident_f[:])
-        nc.vector.memset(b_row[:], 0.0)
-        load_h(0, 2)
+        V.memset(table_seed[:], 0.0)
+        S.activation(out=table_seed[:], in_=table_seed[:], func=ACT.Sigmoid)
+        make_identity(nc, ident_bf16[:])
+        make_identity(nc, ident_f32[:])
+        V.memset(b_rows[:], 0.0)
+
+        load_h(0, 1)
         nc.sync.dma_start(out=q_raw[:], in_=q)
-        load_x(0, 2)
-        nc.sync.dma_start(out=w_raw[:], in_=w_bytes.rearrange("(g p m) n -> p g m n", p=P, m=PACK))
-        nc.sync.dma_start(out=w_sc[:], in_=w_scale.rearrange("(g p m) o -> p g (m o)", p=P, m=PACK))
+        x_in[0] = x_pool.tile([P, 2, D], BF16, name="x")
+        nc.sync.dma_start(out=x_in[0][:, 0, :], in_=x_hbm[:, 0, :])
+        nc.sync.dma_start(out=w_codes_in[:], in_=w_bytes.rearrange("(s p t) n -> p s t n", p=P, t=PACK))
+        nc.sync.dma_start(out=w_scale_in[:], in_=w_scale.rearrange("(s p t) o -> p s (t o)", p=P, t=PACK))
+        nc.sync.dma_start(out=x_in[0][:, 1, :], in_=x_hbm[:, 1, :])
         load_x(1)
-        nc.sync.dma_start(out=b_row[0:2, :], in_=b.rearrange("(o n) -> o n", o=2))
+        load_h(1, 5)
+        nc.sync.dma_start(out=b_rows[0:2, :], in_=b.rearrange("(o n) -> o n", o=2))
         nc.sync.dma_start(out=u_sb[:], in_=u)
         load_x(2)
-        load_h(2, 5)
+        load_h(5, 13)
         load_x(3)
         load_c(0, 2)
 
-        V, S = nc.vector, nc.scalar
         with tc.manual_schedule():
-            h_turn(0)
-            h_copy(0, V.tensor_copy)
-            q_view = q_raw[:].rearrange("k (g p m) -> k g m p", p=P, m=PACK)
-            for g in range(NG):
-                V.tensor_copy(out=q_sb[:, g, :, :], in_=q_view[:, g, :, :])
-            for n in range(NQ + 2):
-                for j in (2 * n + 4, 2 * n + 5):
-                    if j < 2 * NQ:
-                        load_x(j)
+            h_turn(0, 1, "pre")
+            h_copy(0, 1, S.copy)
+            q_view = q_raw[:].rearrange("k (s p t) -> k s t p", p=P, t=PACK)
+            for s in range(PASSES):
+                V.tensor_copy(out=q_sb[:, s, :, :], in_=q_view[:, s, :, :])
+            widen_w(0)
+
+            for n in range(QUADS):
+                for pair in (2 * n + 4, 2 * n + 5):
+                    if pair < 2 * QUADS:
+                        load_x(pair)
                 if n == 1:
-                    load_h(5, 10)
+                    load_h(13, 16)
                     load_c(2, 8)
                 if n == 4:
-                    load_h(10, 16)
                     load_c(8, 16)
-                group(pre_sum, n - 2, 1)
-                quad(h_turn, n + 1)
-                quad(a_mm, n, 0)
-                group(gate, n - 2, 1)
-                quad(a_mm, n, 1)
-                quad(sig, n, 0)
-                quad(h_copy, n + 1, V.tensor_copy)
-                group(pre_sum, n - 2, 0)
-                group(quant, n - 1)
-                quad(sig, n, 1)
-                quad(a_mm, n, 2)
-                group(gate, n - 2, 0)
-                quad(a_mm, n, 3)
-                quad(mult, n, 0)
+
+                quad(a_and_x, n, 0)
+                group(quantize_x1, n - 1)
+                group(add_h_u, n - 2, G_HALF)
+                quad(a_and_x, n, 1)
+                if n == 1:
+                    turn_b()
+                quad(a_and_x, n, 2)
+                if n == 1:
+                    h_turn(5, 2, "pre")
+                quad(sigmoid_a, n, 0)
+                group(gate, n - 2, G_HALF)
+                quad(sigmoid_a, n, 1)
+                quad(sigmoid_a, n, 2)
+                quad(a_and_x, n, 3)
+                group(add_h_u, n - 2, I_HALF)
+                quad(a_and_x, n, 4)
+                quad(a_and_x, n, 5)
                 if n == 0:
-                    widen(0)
-                quad(sig, n, 2)
-                group(mx, n - 1, 1)
-                group(finish, n - 2, nc.gpsimd)
-                quad(sig, n, 3)
-                quad(a_mm, n, 4)
-                group(pre_out, n - 1, 1, "V")
-                quad(a_mm, n, 5)
+                    h_turn(1, 2, "mx")
+                group(mx_product, n - 1, G_HALF)
+                quad(gate_x, n, 0)
                 if n == 0:
-                    bias()
-                quad(sig, n, 4)
-                quad(mult, n, 1)
+                    widen_w(1)
+                quad(sigmoid_a, n, 3)
+                if n == 1:
+                    h_copy(5, 2, S.copy)
+                group(gate, n - 2, I_HALF)
+                quad(sigmoid_a, n, 4)
                 if n == 0:
-                    widen(1)
-                if n == NQ - 1:
-                    quant(NQ - 1)
-                quad(a_mm, n, 6)
-                quad(sig, n, 5)
-                quad(a_mm, n, 7)
-                quad(sig, n, 6)
-                group(mx, n - 1, 0)
-                quad(mult, n, 2)
+                    h_copy(1, 2, S.copy)
+                quad(sigmoid_a, n, 5)
+                quad(gate_x, n, 1)
                 if n == 0:
-                    quant_w()
-                quad(sig, n, 7)
-                group(pre_out, n - 1, 0, "S")
-                quad(mult, n, 3)
-                if n == NQ - 1:
-                    quant(NQ)
-            mx(15, 1)
-            mx(15, 0)
-            pre_out(15, 1, "V")
-            pre_out(15, 0, "S")
-            mx(16, 1)
-            mx(16, 0)
-            pre_out(16, 1, "V")
-            pre_out(16, 0, "S")
-            pre_sum(15, 1)
-            pre_sum(15, 0)
-            gate(15, 1)
-            gate(15, 0)
-            finish(15, nc.gpsimd)
-            pre_sum(16, 1)
-            pre_sum(16, 0)
-            gate(16, 1)
-            gate(16, 0)
-            finish(16, V)
+                    quantize_w()
+                if n == LAST_QUAD:
+                    quantize_x1(PAIR_A)
+                group(mx_copy, n - 1, G_HALF, V)
+                quad(a_and_x, n, 6)
+                if n == 0:
+                    h_turn(3, 2, "pre")
+                if n == 1:
+                    h_turn(7, 2, "pre")
+                quad(a_and_x, n, 7)
+                if n == 4:
+                    h_turn(9, 2, "turn")
+                if n == 6:
+                    h_turn(11, 2, "turn")
+                if n == 7:
+                    h_turn(13, 2, "turn")
+                if n == 10:
+                    h_turn(15, 1, "turn")
+                group(mx_product, n - 1, I_HALF)
+                quad(sigmoid_a, n, 6)
+                quad(gate_x, n, 2)
+                if n == 4:
+                    h_copy(9, 2, V.tensor_copy)
+                if n == 7:
+                    h_copy(13, 2, V.tensor_copy)
+                quad(sigmoid_a, n, 7)
+                if n == 0:
+                    h_copy(3, 2, S.copy)
+                if n == 1:
+                    h_copy(7, 2, S.copy)
+                if n == 6:
+                    h_copy(11, 2, S.copy)
+                if n == 10:
+                    h_copy(15, 1, S.copy)
+                group(update, n - 2, nc.gpsimd)
+                group(mx_copy, n - 1, I_HALF, S)
+                quad(gate_x, n, 3)
+                if n == LAST_QUAD:
+                    quantize_x1(PAIR_B)
+
+            mx_product(PAIR_A, G_HALF, "a")
+            mx_product(PAIR_A, I_HALF, "a")
+            mx_copy(PAIR_A, G_HALF, S)
+            mx_copy(PAIR_A, I_HALF, S)
+            last = PAIR_A - 1
+            add_h_u(last, G_HALF)
+            gate(last, G_HALF)
+            add_h_u(last, I_HALF, "turn")
+            gate(last, I_HALF)
+            update(last, V, (0,), 4)
+            mx_product(PAIR_B, G_HALF, "a")
+            mx_product(PAIR_B, I_HALF, "mx")
+            mx_copy(PAIR_B, G_HALF, V)
+            mx_copy(PAIR_B, I_HALF, S)
+            update(last, V, (1,), 4)
+            add_h_u(PAIR_A, G_HALF, "turn")
+            add_h_u(PAIR_A, I_HALF, "turn")
+            gate(PAIR_A, G_HALF)
+            gate(PAIR_A, I_HALF)
+            update(PAIR_A, V, (0,))
+            update(last, V, (2,), 4)
+            add_h_u(PAIR_B, G_HALF, "pre")
+            add_h_u(PAIR_B, I_HALF, "turn")
+            gate(PAIR_B, G_HALF)
+            gate(PAIR_B, I_HALF)
+            update(PAIR_B, V, (0,))
+            update(PAIR_A, V, (1,))
+            update(PAIR_B, V, (1,))
+            update(PAIR_A, V, (2,))
+            update(PAIR_B, V, (2,))

from contextlib import ExitStack

import concourse.mybir as mybir
from concourse.masks import make_identity

F32 = mybir.dt.float32
BF16 = mybir.dt.bfloat16
U32 = mybir.dt.uint32
U8 = mybir.dt.uint8
FP8 = mybir.dt.float8_e4m3fn
FP8X4 = mybir.dt.float8_e4m3fn_x4
ACT = mybir.ActivationFunctionType
ALU = mybir.AluOpType

P = 128
N, D, H = 8192, 1024, 128
GATES = 2 * H
TILES = N // P
QUADS = TILES // 4
PACK = 4
K_PASS = P * PACK
PASSES = D // K_PASS
FLOPS = 2 * N * (H * D + H * GATES + D * GATES)

GROUPS = [(4 * i, 4) for i in range(QUADS - 1)] + [(TILES - 4, 2), (TILES - 2, 2)]
LAST_QUAD = QUADS - 1
PAIR_A, PAIR_B = QUADS - 1, QUADS

I_HALF, G_HALF = 0, 1


def tile_mogrifieroneroundcoupledlstmcell_t_kernel(tc, x, h, c, q, w_bytes, w_scale, u, b, out):
    nc = tc.nc
    V, S = nc.vector, nc.scalar
    x_hbm = x.rearrange("(p j) d -> p j d", p=P)
    h_hbm = h.rearrange("(p j) d -> p j d", p=P)
    c_hbm = c.rearrange("(p j) d -> p j d", p=P)
    out_hbm = out.rearrange("(p j) d -> p j d", p=P)

    with ExitStack() as ctx:
        keep = ctx.enter_context(tc.tile_pool(name="keep", bufs=1))
        x_pool = ctx.enter_context(tc.tile_pool(name="x_pool", bufs=6))
        work = ctx.enter_context(tc.tile_pool(name="work", bufs=3))
        sig_pool = ctx.enter_context(tc.tile_pool(name="sig_pool", bufs=4))
        banks = {
            "a": ctx.enter_context(tc.psum_pool(name="psum_a", bufs=3)),
            "turn": ctx.enter_context(tc.psum_pool(name="psum_turn", bufs=3)),
            "mx": ctx.enter_context(tc.psum_pool(name="psum_mx", bufs=1)),
            "pre": ctx.enter_context(tc.psum_pool(name="psum_pre", bufs=1)),
        }

        ident_f32 = keep.tile([P, P], F32, name="ident_f32")
        ident_bf16 = keep.tile([P, P], BF16, name="ident_bf16")
        b_rows = keep.tile([P, P], BF16, name="b_rows")
        b_cols = keep.tile([P, 2], F32, name="b_cols")
        q_raw = keep.tile([P, D], BF16, name="q_raw")
        q_sb = keep.tile([P, PASSES, PACK, P], BF16, name="q_sb")
        u_sb = keep.tile([P, GATES], BF16, name="u_sb")
        w_codes_in = keep.tile([P, PASSES, PACK, GATES], U8, name="w_codes_in", align_bytes=64)
        w_scale_in = keep.tile([P, PASSES, PACK], F32, name="w_scale_in")
        w_wide = keep.tile([P, PASSES, PACK, GATES], BF16, name="w_wide")
        w_grouped = keep.tile([P, PASSES, GATES, PACK], BF16, name="w_grouped", align_bytes=64)
        w_mx = keep.tile([P, PASSES * GATES], U32, name="w_mx", align_bytes=64)
        w_mx_scale = keep.tile([P, PASSES * GATES], U8, name="w_mx_scale", align_bytes=64)
        table_seed = keep.tile([P, 1], F32, name="table_seed")

        x_in, h_in, c_in, h_psum, h_t, a_psum, x_psum, sig_a = {}, {}, {}, {}, {}, {}, {}, {}
        x1, x1_mx, mx_psum, mx_t, pre_psum, gates, result = {}, {}, {}, {}, {}, {}, {}

        def load_h(lo, hi):
            t = keep.tile([P, (hi - lo) * 4, H], BF16, name="h%d" % lo)
            nc.sync.dma_start(out=t[:], in_=h_hbm[:, 4 * lo : 4 * hi, :])
            for i in range(lo, hi):
                h_in[i] = t[:, 4 * (i - lo) : 4 * (i - lo) + 4, :]

        def load_c(lo, hi):
            t = keep.tile([P, (hi - lo) * 4, H], BF16, name="c%d" % lo)
            nc.sync.dma_start(out=t[:], in_=c_hbm[:, 4 * lo : 4 * hi, :])
            for j in range(4 * lo, 4 * hi, 2):
                c_in[j] = (t, j - 4 * lo)

        def load_x(pair):
            t = x_pool.tile([P, 2, D], BF16, name="x")
            nc.sync.dma_start(out=t[:], in_=x_hbm[:, 2 * pair : 2 * pair + 2, :])
            x_in[pair] = t

        def h_turn(lo, n, bank):
            t = banks[bank].tile([P, 4 * n, P], BF16, name=bank)
            for i in range(n):
                for j in range(4):
                    nc.tensor.transpose(t[:, 4 * i + j, :], h_in[lo + i][:, j, :], ident_bf16[:])
            h_psum[lo] = t

        def h_copy(lo, n, copy):
            t = keep.tile([P, 4 * n, P], BF16, name="ht%d" % lo)
            copy(out=t[:], in_=h_psum[lo][:])
            for i in range(n):
                h_t[lo + i] = t[:, 4 * i : 4 * i + 4, :]

        def a_and_x(i, k):
            pair, s, m = k // 4, k // 2 % 2, k % 2
            if m == 0:
                x_psum[(i, k // 2)] = banks["turn"].tile([P, 2, 2 * P], F32, name="turn")
            turned = x_psum[(i, k // 2)]
            words = x_in[2 * i + pair][:].bitcast(F32)
            t = banks["a"].tile([P, 2, 2 * P], F32, name="a")
            for e in range(2):
                nc.tensor.transpose(
                    turned[:, e, P * m : P * m + P],
                    words[:, m, 256 * s + e : 256 * s + 256 : 2],
                    ident_f32[:],
                )
                nc.tensor.matmul(
                    t[:, e, :],
                    lhsT=q_sb[:, s, 2 * m + e, :],
                    rhs=h_t[i][:, 2 * pair : 2 * pair + 2, :].rearrange("p j n -> p (j n)"),
                    start=True,
                    stop=True,
                )
            a_psum[(i, k)] = t

        def sigmoid_a(i, k):
            if k % 2 == 0:
                sig_a[(i, k // 2)] = sig_pool.tile([P, 2, 2 * P, 2], F32, name="sig")
            S.activation(
                out=sig_a[(i, k // 2)][:, k % 2, :, :],
                in_=a_psum[(i, k)][:].rearrange("p e n -> p n e"),
                func=ACT.Sigmoid,
            )

        def gate_x(i, k):
            pair, s = k // 2, k % 2
            j, place = (i, pair) if i < LAST_QUAD else (PAIR_A + pair, 0)
            if j not in x1:
                x1[j] = work.tile([P, PASSES, GROUPS[j][1] * K_PASS], BF16, name="x1", align_bytes=64)
            V.tensor_tensor(
                out=x1[j][:, s, 1024 * place : 1024 * place + 1024].rearrange("p (n m e) -> p n m e", m=2, e=2),
                in0=x_psum[(i, k)][:].bitcast(BF16).rearrange("p m (n e) -> p n m e", e=2),
                in1=sig_a[(i, k)][:].rearrange("p m n e -> p n m e"),
                op=ALU.mult,
            )

        def quantize_x1(j):
            words = PASSES * GROUPS[j][1] * P
            codes = work.tile([P, words], U32, name="x1_mx", align_bytes=64)
            scales = work.tile([P, words], U8, name="x1_mx_scale", align_bytes=64)
            V.quantize_mx(
                out=codes[:].bitcast(FP8X4), scales=scales[:], in_=x1[j][:].rearrange("p s m -> p (s m)")
            )
            x1_mx[j] = (codes, scales)

        def mx_product(j, half, bank="mx"):
            tokens = GROUPS[j][1] * P
            t = banks[bank].tile([P, tokens], F32, name=bank)
            codes, scales = x1_mx[j]
            for s in range(PASSES):
                w_cols = slice(s * GATES + half * P, s * GATES + half * P + P)
                x_cols = slice(s * tokens, s * tokens + tokens)
                nc.tensor.matmul_mx(
                    out=t[:],
                    lhsT=w_mx[:, w_cols].bitcast(FP8X4),
                    lhsT_scale=w_mx_scale[:, w_cols],
                    rhs=codes[:, x_cols].bitcast(FP8X4),
                    rhs_scale=scales[:, x_cols],
                    start=(s == 0),
                    stop=(s == PASSES - 1),
                )
            mx_psum[(j, half)] = t

        def mx_copy(j, half, engine):
            t = work.tile([P, GROUPS[j][1] * P], F32, name="mx_t%d" % half)
            b_col = b_cols[:, half : half + 1]
            if engine is S:
                S.activation(out=t[:], in_=mx_psum[(j, half)][:], func=ACT.Identity, bias=b_col, scale=2.0)
            else:
                V.tensor_scalar(
                    out=t[:], in0=mx_psum[(j, half)][:], scalar1=2.0, scalar2=b_col, op0=ALU.mult, op1=ALU.add
                )
            mx_t[(j, half)] = t

        def add_h_u(j, half, bank="pre"):
            first, n = GROUPS[j]
            t = banks[bank].tile([P, n, P], F32, name=bank)
            for k in range(n):
                i, tile = (first + k) // 4, (first + k) % 4
                nc.tensor.matmul(
                    t[:, k, :],
                    lhsT=h_t[i][:, tile, :],
                    rhs=u_sb[:, P * half : P * half + P],
                    start=(k == 0),
                    stop=False,
                )
            for k in range(n):
                nc.tensor.matmul(
                    t[:, k, :],
                    lhsT=mx_t[(j, half)][:, P * k : P * k + P],
                    rhs=ident_f32[:],
                    is_transpose=True,
                    start=False,
                    stop=(k == n - 1),
                )
            pre_psum[(j, half)] = t

        def gate(j, half):
            t = keep.tile([P, GROUPS[j][1], H], F32, name="gate%d_%d" % (half, j))
            S.activation(out=t[:], in_=pre_psum[(j, half)][:], func=ACT.Tanh if half == G_HALF else ACT.Sigmoid)
            gates[(j, half)] = t

        def update(j, engine, steps=(0, 1, 2), tiles=2):
            first, n = GROUPS[j]
            i_t, g_t = gates[(j, I_HALF)], gates[(j, G_HALF)]
            c_t, place = c_in[first]
            if 0 in steps:
                result[j] = work.tile([P, n, H], F32, name="result")
            for step in steps:
                for k in range(0, n, tiles):
                    z = slice(k, k + tiles)
                    c_z = c_t[:, place + k : place + k + tiles, :]
                    if step == 0:
                        engine.tensor_tensor(out=g_t[:, z, :], in0=g_t[:, z, :], in1=c_z, op=ALU.subtract)
                    elif step == 1:
                        engine.tensor_tensor(out=i_t[:, z, :], in0=i_t[:, z, :], in1=g_t[:, z, :], op=ALU.mult)
                    else:
                        engine.tensor_tensor(out=result[j][:, z, :], in0=i_t[:, z, :], in1=c_z, op=ALU.add)
            if 2 in steps:
                nc.sync.dma_start(out=out_hbm[:, first : first + n, :], in_=result[j][:])

        def widen_w(s):
            for t in range(PACK):
                V.tensor_scalar(
                    out=w_wide[:, s, t, :],
                    in0=w_codes_in[:, s, t, :].bitcast(FP8),
                    scalar1=w_scale_in[:, s, t : t + 1],
                    scalar2=None,
                    op0=ALU.mult,
                )
            V.tensor_copy(out=w_grouped[:, s, :, :], in_=w_wide[:, s, :, :].rearrange("p t n -> p n t"))

        def quantize_w():
            V.quantize_mx(
                out=w_mx[:].bitcast(FP8X4),
                scales=w_mx_scale[:],
                in_=w_grouped[:].rearrange("p s n t -> p (s n t)"),
            )

        def turn_b():
            t = banks["turn"].tile([P, P], BF16, name="turn")
            nc.tensor.transpose(t[:], b_rows[:], ident_bf16[:])
            V.tensor_copy(out=b_cols[:], in_=t[:, 0:2])

        def quad(step, i, *args):
            if 0 <= i < QUADS:
                step(i, *args)

        def group(step, j, *args):
            if 0 <= j < LAST_QUAD:
                step(j, *args)

        V.memset(table_seed[:], 0.0)
        S.activation(out=table_seed[:], in_=table_seed[:], func=ACT.Sigmoid)
        make_identity(nc, ident_bf16[:])
        make_identity(nc, ident_f32[:])
        V.memset(b_rows[:], 0.0)

        load_h(0, 1)
        nc.sync.dma_start(out=q_raw[:], in_=q)
        x_in[0] = x_pool.tile([P, 2, D], BF16, name="x")
        nc.sync.dma_start(out=x_in[0][:, 0, :], in_=x_hbm[:, 0, :])
        nc.sync.dma_start(out=w_codes_in[:], in_=w_bytes.rearrange("(s p t) n -> p s t n", p=P, t=PACK))
        nc.sync.dma_start(out=w_scale_in[:], in_=w_scale.rearrange("(s p t) o -> p s (t o)", p=P, t=PACK))
        nc.sync.dma_start(out=x_in[0][:, 1, :], in_=x_hbm[:, 1, :])
        load_x(1)
        load_h(1, 5)
        nc.sync.dma_start(out=b_rows[0:2, :], in_=b.rearrange("(o n) -> o n", o=2))
        nc.sync.dma_start(out=u_sb[:], in_=u)
        load_x(2)
        load_h(5, 13)
        load_x(3)
        load_c(0, 2)

        with tc.manual_schedule():
            h_turn(0, 1, "pre")
            h_copy(0, 1, S.copy)
            q_view = q_raw[:].rearrange("k (s p t) -> k s t p", p=P, t=PACK)
            for s in range(PASSES):
                V.tensor_copy(out=q_sb[:, s, :, :], in_=q_view[:, s, :, :])
            widen_w(0)

            for n in range(QUADS):
                for pair in (2 * n + 4, 2 * n + 5):
                    if pair < 2 * QUADS:
                        load_x(pair)
                if n == 1:
                    load_h(13, 16)
                    load_c(2, 8)
                if n == 4:
                    load_c(8, 16)

                quad(a_and_x, n, 0)
                group(quantize_x1, n - 1)
                group(add_h_u, n - 2, G_HALF)
                quad(a_and_x, n, 1)
                if n == 1:
                    turn_b()
                quad(a_and_x, n, 2)
                if n == 1:
                    h_turn(5, 2, "pre")
                quad(sigmoid_a, n, 0)
                group(gate, n - 2, G_HALF)
                quad(sigmoid_a, n, 1)
                quad(sigmoid_a, n, 2)
                quad(a_and_x, n, 3)
                group(add_h_u, n - 2, I_HALF)
                quad(a_and_x, n, 4)
                quad(a_and_x, n, 5)
                if n == 0:
                    h_turn(1, 2, "mx")
                group(mx_product, n - 1, G_HALF)
                quad(gate_x, n, 0)
                if n == 0:
                    widen_w(1)
                quad(sigmoid_a, n, 3)
                if n == 1:
                    h_copy(5, 2, S.copy)
                group(gate, n - 2, I_HALF)
                quad(sigmoid_a, n, 4)
                if n == 0:
                    h_copy(1, 2, S.copy)
                quad(sigmoid_a, n, 5)
                quad(gate_x, n, 1)
                if n == 0:
                    quantize_w()
                if n == LAST_QUAD:
                    quantize_x1(PAIR_A)
                group(mx_copy, n - 1, G_HALF, V)
                quad(a_and_x, n, 6)
                if n == 0:
                    h_turn(3, 2, "pre")
                if n == 1:
                    h_turn(7, 2, "pre")
                quad(a_and_x, n, 7)
                if n == 4:
                    h_turn(9, 2, "turn")
                if n == 6:
                    h_turn(11, 2, "turn")
                if n == 7:
                    h_turn(13, 2, "turn")
                if n == 10:
                    h_turn(15, 1, "turn")
                group(mx_product, n - 1, I_HALF)
                quad(sigmoid_a, n, 6)
                quad(gate_x, n, 2)
                if n == 4:
                    h_copy(9, 2, V.tensor_copy)
                if n == 7:
                    h_copy(13, 2, V.tensor_copy)
                quad(sigmoid_a, n, 7)
                if n == 0:
                    h_copy(3, 2, S.copy)
                if n == 1:
                    h_copy(7, 2, S.copy)
                if n == 6:
                    h_copy(11, 2, S.copy)
                if n == 10:
                    h_copy(15, 1, S.copy)
                group(update, n - 2, nc.gpsimd)
                group(mx_copy, n - 1, I_HALF, S)
                quad(gate_x, n, 3)
                if n == LAST_QUAD:
                    quantize_x1(PAIR_B)

            mx_product(PAIR_A, G_HALF, "a")
            mx_product(PAIR_A, I_HALF, "a")
            mx_copy(PAIR_A, G_HALF, S)
            mx_copy(PAIR_A, I_HALF, S)
            last = PAIR_A - 1
            add_h_u(last, G_HALF)
            gate(last, G_HALF)
            add_h_u(last, I_HALF, "turn")
            gate(last, I_HALF)
            update(last, V, (0,), 4)
            mx_product(PAIR_B, G_HALF, "a")
            mx_product(PAIR_B, I_HALF, "mx")
            mx_copy(PAIR_B, G_HALF, V)
            mx_copy(PAIR_B, I_HALF, S)
            update(last, V, (1,), 4)
            add_h_u(PAIR_A, G_HALF, "turn")
            add_h_u(PAIR_A, I_HALF, "turn")
            gate(PAIR_A, G_HALF)
            gate(PAIR_A, I_HALF)
            update(PAIR_A, V, (0,))
            update(last, V, (2,), 4)
            add_h_u(PAIR_B, G_HALF, "pre")
            add_h_u(PAIR_B, I_HALF, "turn")
            gate(PAIR_B, G_HALF)
            gate(PAIR_B, I_HALF)
            update(PAIR_B, V, (0,))
            update(PAIR_A, V, (1,))
            update(PAIR_B, V, (1,))
            update(PAIR_A, V, (2,))
            update(PAIR_B, V, (2,))
